import numpy as np
import ml_dtypes


def mxq(x, axis, fmt="e4m3"):
    dtype, down = {"e4m3": (ml_dtypes.float8_e4m3fn, 7), "e5m2": (ml_dtypes.float8_e5m2, 14)}[fmt]
    v = np.moveaxis(np.asarray(x, np.float32).astype(ml_dtypes.bfloat16).astype(np.float64), axis, -1)
    blocks = v.reshape(v.shape[:-1] + (-1, 32))
    amax = np.abs(blocks).max(-1, keepdims=True)
    byte = np.maximum(np.where(amax > 0, np.frexp(amax)[1] - 1 + 127, 0) - down, 1)
    scale = np.exp2(byte - 127.0)
    codes = (blocks / scale).astype(np.float32).astype(dtype).astype(np.float64)
    return np.moveaxis((codes * scale).reshape(v.shape), -1, axis)


WIDE = False


def mx_kscale(k):
    if not WIDE:
        return np.ones(k)
    levels = np.array([10, -10, 5, -5, 0])
    if k % 512:
        return np.exp2(np.random.permutation(np.resize(levels, k // 32))).repeat(32)
    a = np.empty((k // 512, 16))
    for p in range(k // 512):
        a[p, :8] = np.random.permutation(np.resize(levels, 8))
        for g in range(8):
            far = levels[np.abs(levels - a[p, g]) >= 10]
            a[p, g + 8] = far[np.random.randint(len(far))]
    return np.exp2(a.ravel()).repeat(32)


def f64(x):
    return np.asarray(x).astype(np.float64)


def striped(idx):
    return np.tile(np.asarray(idx).reshape(-1, 16).T, (8, 1)).astype(np.uint16)


def unstriped(offs):
    return offs[:16].T.reshape(-1).astype(np.int64)


E2M1 = np.array([0.0, 0.5, 1.0, 1.5, 2.0, 3.0, 4.0, 6.0, -0.0, -0.5, -1.0, -1.5, -2.0, -3.0, -4.0, -6.0])


def pack_weight(w, fmt):
    k, n = w.shape
    w = f64(np.asarray(w, np.float32).astype(ml_dtypes.bfloat16)).reshape(k // 32, 32, n)
    amax = np.abs(w).max(1)
    if fmt == "e4m3":
        byte = np.frexp(amax)[1] - 1 + 127 - 7
    else:
        mant, ex = np.frexp(amax / 6.0)
        byte = np.where(mant > 0.5, ex, ex - 1) + 127
    byte = np.clip(np.where(amax > 0, byte, 1), 1, 254)
    scaled = (w * np.exp2(127.0 - byte)[:, None, :]).reshape(k, n).astype(np.float32)
    by_word = np.ascontiguousarray(scaled.reshape(k // 512, 128, 4, n).transpose(0, 1, 3, 2))
    if fmt == "e4m3":
        words = by_word.astype(ml_dtypes.float8_e4m3fn).view(np.uint8)
    else:
        c = by_word.astype(ml_dtypes.float4_e2m1fn).view(np.uint8) & 0xF
        words = (c[..., 0::2] | (c[..., 1::2] << 4)).reshape(k // 512, 128, 2 * n)
    return np.ascontiguousarray(words), np.ascontiguousarray(byte.astype(np.uint8).reshape(k // 512, 16, n))


def unpack_weight(words, scales, fmt):
    g, _, n = scales.shape
    words = np.ascontiguousarray(words).reshape(g, 128, n, -1)
    if fmt == "e4m3":
        vals = words.view(ml_dtypes.float8_e4m3fn).astype(np.float64)
    else:
        nib = np.empty((g, 128, n, 4), np.uint8)
        nib[..., 0::2] = words & 0xF
        nib[..., 1::2] = words >> 4
        vals = E2M1[nib]
    vals = vals * np.repeat(np.exp2(scales.astype(np.float64) - 127.0), 8, axis=1)[..., None]
    return vals.transpose(0, 1, 3, 2).reshape(g * 512, n)


D, K, T, I, Q = 1024, 512, 2048, 512, 128


def setup_inputs():
    n = np.random.standard_normal
    idx = np.random.permutation(T)[:I]
    fd = mx_kscale(D)
    fk = mx_kscale(K)
    etp = pack_weight(n((D, T)) / fd[:, None], "e2m1")
    edp = pack_weight(n((K, T)) / fk[:, None], "e4m3")
    return {
        "ht": (n((D, Q)) * 1.0 / np.sqrt(D) * fd[:, None]).astype(np.float32),
        "hd": (n((K, Q)) * 1.0 / np.sqrt(K) * fk[:, None]).astype(np.float32),
        "et_words": etp[0],
        "et_scales": etp[1],
        "ed_words": edp[0],
        "ed_scales": edp[1],
        "l1": (np.random.uniform(6.6, 6.9, (Q, 1))).astype(np.float32),
        "l2": (np.random.uniform(6.6, 6.9, (Q, 1))).astype(np.float32),
        "offs": striped(idx),
    }


def reference(ht, hd, et_words, et_scales, ed_words, ed_scales, l1, l2, offs):
    idx = unstriped(offs)
    etu = unpack_weight(et_words, et_scales, "e2m1")
    edu = unpack_weight(ed_words, ed_scales, "e4m3")
    htq = mxq(f64(ht), 0, "e4m3")
    etidxg = etu[:, idx]
    a = htq.T @ etidxg
    hdq = mxq(f64(hd), 0, "e4m3")
    edidxg = edu[:, idx]
    b = hdq.T @ edidxg
    y = np.minimum(np.exp(a - f64(l1) - b + f64(l2)), 1.0)
    return y

@@ -1,0 +1,135 @@
+from contextlib import ExitStack
+
+import concourse.mybir as mybir
+
+D, K, T, I, Q = 1024, 512, 2048, 512, 128
+FLOPS = 2 * (D + K) * Q * I
+
+F32 = mybir.dt.float32
+BF16 = mybir.dt.bfloat16
+I32 = mybir.dt.int32
+U32 = mybir.dt.uint32
+U16 = mybir.dt.uint16
+U8 = mybir.dt.uint8
+FP8X4 = mybir.dt.float8_e4m3fn_x4
+FP4X4 = mybir.dt.float4_e2m1fn_x4
+ACT = mybir.ActivationFunctionType
+ALU = mybir.AluOpType
+
+P = 128
+PACK = 4
+N = 128
+
+
+def tile_attend_speculate_accept_kernel(tc, ht, hd, et_words, et_scales, ed_words, ed_scales, l1, l2, offs, out):
+    nc = tc.nc
+    with ExitStack() as ctx:
+        sb = ctx.enter_context(tc.tile_pool(name="sb", bufs=1))
+        ps = ctx.enter_context(tc.psum_pool(name="ps", bufs=1))
+
+        offsets = sb.tile([P, I // 16], U16, name="offsets")
+        et_win = [sb.tile([P, T], U16, name=f"et_win{z}", align_bytes=64) for z in range(2)]
+        ed_win = sb.tile([P, T], U32, name="ed_win", align_bytes=64)
+        ets_win = sb.tile([P, 2, T], U8, name="ets_win", align_bytes=64)
+        eds_win = sb.tile([P, T], U8, name="eds_win", align_bytes=64)
+        ht_raw = sb.tile([P, 2, PACK, Q], F32, name="ht_raw", align_bytes=64)
+        hd_raw = sb.tile([P, PACK, Q], F32, name="hd_raw", align_bytes=64)
+        l1_col = sb.tile([P, 1], F32, name="l1_col")
+        l2_col = sb.tile([P, 1], F32, name="l2_col")
+
+        nc.vector.memset(ets_win[:].bitcast(I32), 0)
+        nc.vector.memset(eds_win[:].bitcast(I32), 0)
+
+        nc.gpsimd.dma_start(l1_col[:], l1)
+        nc.gpsimd.dma_start(l2_col[:], l2)
+
+        nc.sync.dma_start(offsets[:], offs)
+        nc.sync.dma_start(et_win[0][:].bitcast(I32), et_words[0].bitcast(I32))
+        for quad in range(4):
+            nc.sync.dma_start(
+                ets_win[32 * quad : 32 * quad + 4].bitcast(I32),
+                et_scales[:, 4 * quad : 4 * quad + 4, :].rearrange("z r c -> r z c").bitcast(I32),
+            )
+        nc.sync.dma_start(et_win[1][:].bitcast(I32), et_words[1].bitcast(I32))
+        nc.sync.dma_start(ht_raw[:], ht.rearrange("(z p j) q -> p z j q", z=2, j=PACK))
+        nc.sync.dma_start(hd_raw[:], hd.rearrange("(p j) q -> p j q", j=PACK))
+        for quad in range(4):
+            nc.sync.dma_start(
+                eds_win[32 * quad : 32 * quad + 4].bitcast(I32),
+                ed_scales[0, 4 * quad : 4 * quad + 4, :].bitcast(I32),
+            )
+        nc.sync.dma_start(ed_win[:].bitcast(I32), ed_words[0].rearrange("p c r -> p (c r)").bitcast(I32))
+
+        shift = sb.tile([P, 1], F32, name="shift")
+        nc.scalar.activation(shift[:], l2_col[:], ACT.Identity, bias=l1_col[:], scale=-1.0)
+
+        ht_bf = sb.tile([P, 2, Q, PACK], BF16, name="ht_bf", align_bytes=64)
+        hd_bf = sb.tile([P, Q, PACK], BF16, name="hd_bf", align_bytes=64)
+        for z in range(2):
+            nc.scalar.activation(
+                ht_bf[:, z].rearrange("p (c i) j -> p c j i", i=4),
+                ht_raw[:, z].rearrange("p j (c i) -> p c j i", i=4),
+                ACT.Copy,
+                scale=-1.0,
+            )
+        nc.scalar.activation(
+            hd_bf[:].rearrange("p (c i) j -> p c j i", i=4),
+            hd_raw[:].rearrange("p j (c i) -> p c j i", i=4),
+            ACT.Copy,
+        )
+
+        et_g = [sb.tile([P, I], U16, name=f"et_g{z}", align_bytes=64) for z in range(2)]
+        ets_g = [sb.tile([P, I], U8, name=f"ets_g{z}", align_bytes=64) for z in range(2)]
+        eds_g = sb.tile([P, I], U8, name="eds_g", align_bytes=64)
+        ed_g = [sb.tile([P, I // 2], U32, name=f"ed_g{h}", align_bytes=64) for h in range(2)]
+        ht_c = sb.tile([P, 2 * Q], U32, name="ht_c", align_bytes=64)
+        ht_s = sb.tile([P, 2 * Q], U8, name="ht_s", align_bytes=64)
+        hd_c = sb.tile([P, Q], U32, name="hd_c", align_bytes=64)
+        hd_s = sb.tile([P, Q], U8, name="hd_s", align_bytes=64)
+
+        nc.vector.tensor_copy(et_g[0][:], et_win[0][:].indirect(offsets[:]))
+        for z in range(2):
+            nc.vector.tensor_copy(ets_g[z][:], ets_win[:, z].indirect(offsets[:]))
+        nc.vector.tensor_copy(et_g[1][:], et_win[1][:].indirect(offsets[:]))
+        nc.vector.quantize_mx(ht_c[:].bitcast(FP8X4), ht_s[:], ht_bf[:].rearrange("p z q j -> p (z q j)"))
+        nc.vector.tensor_copy(eds_g[:], eds_win[:].indirect(offsets[:]))
+        nc.vector.quantize_mx(hd_c[:].bitcast(FP8X4), hd_s[:], hd_bf[:].rearrange("p q j -> p (q j)"))
+
+        banks = [ps.tile([P, N], F32, name=f"bank{b}") for b in range(I // N)]
+        for z in range(2):
+            for b in range(I // N):
+                cols = slice(b * N, (b + 1) * N)
+                nc.tensor.matmul_mx(
+                    banks[b][:],
+                    lhsT=ht_c[:, z * Q : (z + 1) * Q].bitcast(FP8X4),
+                    lhsT_scale=ht_s[:, z * Q : (z + 1) * Q],
+                    rhs=et_g[z][:, cols].bitcast(FP4X4),
+                    rhs_scale=ets_g[z][:, cols],
+                    start=(z == 0),
+                    stop=False,
+                )
+
+        for h in range(2):
+            nc.vector.tensor_copy(ed_g[h][:], ed_win[:].indirect(offsets[:, h * 16 : (h + 1) * 16]))
+        for h in range(2):
+            excess = sb.tile([P, 2 * N], F32, name=f"excess{h}")
+            chance = sb.tile([P, 2 * N], F32, name=f"chance{h}")
+            for u in range(2):
+                b = 2 * h + u
+                nc.tensor.matmul_mx(
+                    banks[b][:],
+                    lhsT=hd_c[:].bitcast(FP8X4),
+                    lhsT_scale=hd_s[:],
+                    rhs=ed_g[h][:, u * N : (u + 1) * N].bitcast(FP8X4),
+                    rhs_scale=eds_g[:, b * N : (b + 1) * N],
+                    start=False,
+                    stop=True,
+                )
+                if h == 0:
+                    nc.scalar.activation(excess[:, u * N : (u + 1) * N], banks[b][:], ACT.Relu, bias=shift[:])
+                else:
+                    nc.vector.tensor_scalar(
+                        excess[:, u * N : (u + 1) * N], banks[b][:], shift[:], 0.0, op0=ALU.add, op1=ALU.max
+                    )
+            nc.scalar.activation(chance[:], excess[:], ACT.Exp, scale=-1.0)
+            nc.sync.dma_start(out[:, h * 2 * N : (h + 1) * 2 * N], chance[:])

@@ -30,8 +30,8 @@ def tile_attend_speculate_accept_kernel(tc, ht, hd, et_words, et_scales, ed_word
         offsets = sb.tile([P, I // 16], U16, name="offsets")
         et_win = [sb.tile([P, T], U16, name=f"et_win{z}", align_bytes=64) for z in range(2)]
         ed_win = sb.tile([P, T], U32, name="ed_win", align_bytes=64)
-        ets_win = sb.tile([P, 2, T], U8, name="ets_win", align_bytes=64)
-        eds_win = sb.tile([P, T], U8, name="eds_win", align_bytes=64)
+        ets_win = sb.tile([P, T], U8, name="ets_win", align_bytes=64)
+        eds_win = sb.tile([P, T], U8, name="eds_win", tag="eds_then_ht", align_bytes=64)
         ht_raw = sb.tile([P, 2, PACK, Q], F32, name="ht_raw", align_bytes=64)
         hd_raw = sb.tile([P, PACK, Q], F32, name="hd_raw", align_bytes=64)
         l1_col = sb.tile([P, 1], F32, name="l1_col")
@@ -39,29 +39,31 @@ def tile_attend_speculate_accept_kernel(tc, ht, hd, et_words, et_scales, ed_word
 
         nc.vector.memset(ets_win[:].bitcast(I32), 0)
         nc.vector.memset(eds_win[:].bitcast(I32), 0)
+        warm = sb.tile([P, 2], F32, name="warm")
+        nc.gpsimd.memset(warm[:, 0:1], 0.0)
+        nc.scalar.activation(warm[:, 1:2], warm[:, 0:1], ACT.Exp)
+        ets_g = [sb.tile([P, I], U8, name=f"ets_g{z}", align_bytes=64) for z in range(2)]
+        nc.gpsimd.memset(ets_g[1][:].bitcast(I32), 0)
 
         nc.gpsimd.dma_start(l1_col[:], l1)
         nc.gpsimd.dma_start(l2_col[:], l2)
 
         nc.sync.dma_start(offsets[:], offs)
         nc.sync.dma_start(et_win[0][:].bitcast(I32), et_words[0].bitcast(I32))
-        for quad in range(4):
+        for r in range(4):
             nc.sync.dma_start(
-                ets_win[32 * quad : 32 * quad + 4].bitcast(I32),
-                et_scales[:, 4 * quad : 4 * quad + 4, :].rearrange("z r c -> r z c").bitcast(I32),
+                ets_win[r:P:16].bitcast(I32),
+                et_scales[:, r:16:4, :].rearrange("z a c -> a z c").bitcast(I32),
             )
         nc.sync.dma_start(et_win[1][:].bitcast(I32), et_words[1].bitcast(I32))
         nc.sync.dma_start(ht_raw[:], ht.rearrange("(z p j) q -> p z j q", z=2, j=PACK))
+        for r in range(4):
+            nc.sync.dma_start(eds_win[r:P:32].bitcast(I32), ed_scales[0, r:16:4, :].bitcast(I32))
         nc.sync.dma_start(hd_raw[:], hd.rearrange("(p j) q -> p j q", j=PACK))
-        for quad in range(4):
-            nc.sync.dma_start(
-                eds_win[32 * quad : 32 * quad + 4].bitcast(I32),
-                ed_scales[0, 4 * quad : 4 * quad + 4, :].bitcast(I32),
-            )
         nc.sync.dma_start(ed_win[:].bitcast(I32), ed_words[0].rearrange("p c r -> p (c r)").bitcast(I32))
 
         shift = sb.tile([P, 1], F32, name="shift")
-        nc.scalar.activation(shift[:], l2_col[:], ACT.Identity, bias=l1_col[:], scale=-1.0)
+        nc.gpsimd.tensor_tensor(shift[:], l1_col[:], l2_col[:], ALU.subtract)
 
         ht_bf = sb.tile([P, 2, Q, PACK], BF16, name="ht_bf", align_bytes=64)
         hd_bf = sb.tile([P, Q, PACK], BF16, name="hd_bf", align_bytes=64)
@@ -79,25 +81,24 @@ def tile_attend_speculate_accept_kernel(tc, ht, hd, et_words, et_scales, ed_word
         )
 
         et_g = [sb.tile([P, I], U16, name=f"et_g{z}", align_bytes=64) for z in range(2)]
-        ets_g = [sb.tile([P, I], U8, name=f"ets_g{z}", align_bytes=64) for z in range(2)]
         eds_g = sb.tile([P, I], U8, name="eds_g", align_bytes=64)
         ed_g = [sb.tile([P, I // 2], U32, name=f"ed_g{h}", align_bytes=64) for h in range(2)]
-        ht_c = sb.tile([P, 2 * Q], U32, name="ht_c", align_bytes=64)
+        ht_c = sb.tile([P, 2 * Q], U32, name="ht_c", tag="eds_then_ht", align_bytes=64)
         ht_s = sb.tile([P, 2 * Q], U8, name="ht_s", align_bytes=64)
         hd_c = sb.tile([P, Q], U32, name="hd_c", align_bytes=64)
         hd_s = sb.tile([P, Q], U8, name="hd_s", align_bytes=64)
 
         nc.vector.tensor_copy(et_g[0][:], et_win[0][:].indirect(offsets[:]))
-        for z in range(2):
-            nc.vector.tensor_copy(ets_g[z][:], ets_win[:, z].indirect(offsets[:]))
+        nc.vector.tensor_copy(ets_g[0][:], ets_win[:].indirect(offsets[:]))
+        nc.scalar.dma_start(ets_g[1][0:100].bitcast(I32), ets_g[0][16:116].bitcast(I32))
         nc.vector.tensor_copy(et_g[1][:], et_win[1][:].indirect(offsets[:]))
-        nc.vector.quantize_mx(ht_c[:].bitcast(FP8X4), ht_s[:], ht_bf[:].rearrange("p z q j -> p (z q j)"))
         nc.vector.tensor_copy(eds_g[:], eds_win[:].indirect(offsets[:]))
+        nc.vector.quantize_mx(ht_c[:].bitcast(FP8X4), ht_s[:], ht_bf[:].rearrange("p z q j -> p (z q j)"))
         nc.vector.quantize_mx(hd_c[:].bitcast(FP8X4), hd_s[:], hd_bf[:].rearrange("p q j -> p (q j)"))
 
         banks = [ps.tile([P, N], F32, name=f"bank{b}") for b in range(I // N)]
-        for z in range(2):
-            for b in range(I // N):
+        for b, z in [(2 * h + u, z) for h in range(2) for z in range(2) for u in range(2)]:
+            if True:
                 cols = slice(b * N, (b + 1) * N)
                 nc.tensor.matmul_mx(
                     banks[b][:],

@@ -28,10 +28,10 @@ def tile_attend_speculate_accept_kernel(tc, ht, hd, et_words, et_scales, ed_word
         ps = ctx.enter_context(tc.psum_pool(name="ps", bufs=1))
 
         offsets = sb.tile([P, I // 16], U16, name="offsets")
-        et_win = [sb.tile([P, T], U16, name=f"et_win{z}", align_bytes=64) for z in range(2)]
+        et_win = [sb.tile([P, T], U16, name=f"et_win{z}", tag=f"et_win{z}", align_bytes=64) for z in range(2)]
         ed_win = sb.tile([P, T], U32, name="ed_win", align_bytes=64)
         ets_win = sb.tile([P, T], U8, name="ets_win", align_bytes=64)
-        eds_win = sb.tile([P, T], U8, name="eds_win", tag="eds_then_ht", align_bytes=64)
+        eds_win = sb.tile([P, T], U8, name="eds_win", align_bytes=64)
         ht_raw = sb.tile([P, 2, PACK, Q], F32, name="ht_raw", align_bytes=64)
         hd_raw = sb.tile([P, PACK, Q], F32, name="hd_raw", align_bytes=64)
         l1_col = sb.tile([P, 1], F32, name="l1_col")
@@ -48,17 +48,17 @@ def tile_attend_speculate_accept_kernel(tc, ht, hd, et_words, et_scales, ed_word
         nc.gpsimd.dma_start(l1_col[:], l1)
         nc.gpsimd.dma_start(l2_col[:], l2)
 
-        nc.sync.dma_start(offsets[:], offs)
         nc.sync.dma_start(et_win[0][:].bitcast(I32), et_words[0].bitcast(I32))
+        nc.sync.dma_start(offsets[:], offs)
         for r in range(4):
             nc.sync.dma_start(
                 ets_win[r:P:16].bitcast(I32),
                 et_scales[:, r:16:4, :].rearrange("z a c -> a z c").bitcast(I32),
             )
-        nc.sync.dma_start(et_win[1][:].bitcast(I32), et_words[1].bitcast(I32))
         nc.sync.dma_start(ht_raw[:], ht.rearrange("(z p j) q -> p z j q", z=2, j=PACK))
+        nc.sync.dma_start(et_win[1][:].bitcast(I32), et_words[1].bitcast(I32))
         for r in range(4):
-            nc.sync.dma_start(eds_win[r:P:32].bitcast(I32), ed_scales[0, r:16:4, :].bitcast(I32))
+            nc.sync.dma_start(eds_win[4 + r : P : 32].bitcast(I32), ed_scales[0, r:16:4, :].bitcast(I32))
         nc.sync.dma_start(hd_raw[:], hd.rearrange("(p j) q -> p j q", j=PACK))
         nc.sync.dma_start(ed_win[:].bitcast(I32), ed_words[0].rearrange("p c r -> p (c r)").bitcast(I32))
 
@@ -83,22 +83,22 @@ def tile_attend_speculate_accept_kernel(tc, ht, hd, et_words, et_scales, ed_word
         et_g = [sb.tile([P, I], U16, name=f"et_g{z}", align_bytes=64) for z in range(2)]
         eds_g = sb.tile([P, I], U8, name="eds_g", align_bytes=64)
         ed_g = [sb.tile([P, I // 2], U32, name=f"ed_g{h}", align_bytes=64) for h in range(2)]
-        ht_c = sb.tile([P, 2 * Q], U32, name="ht_c", tag="eds_then_ht", align_bytes=64)
+        ht_c = sb.tile([P, 2 * Q], U32, name="ht_c", align_bytes=64)
         ht_s = sb.tile([P, 2 * Q], U8, name="ht_s", align_bytes=64)
         hd_c = sb.tile([P, Q], U32, name="hd_c", align_bytes=64)
         hd_s = sb.tile([P, Q], U8, name="hd_s", align_bytes=64)
 
         nc.vector.tensor_copy(et_g[0][:], et_win[0][:].indirect(offsets[:]))
         nc.vector.tensor_copy(ets_g[0][:], ets_win[:].indirect(offsets[:]))
-        nc.scalar.dma_start(ets_g[1][0:100].bitcast(I32), ets_g[0][16:116].bitcast(I32))
+        nc.sync.dma_start(ets_g[1][0:100].bitcast(I32), ets_g[0][16:116].bitcast(I32))
         nc.vector.tensor_copy(et_g[1][:], et_win[1][:].indirect(offsets[:]))
-        nc.vector.tensor_copy(eds_g[:], eds_win[:].indirect(offsets[:]))
         nc.vector.quantize_mx(ht_c[:].bitcast(FP8X4), ht_s[:], ht_bf[:].rearrange("p z q j -> p (z q j)"))
+        nc.vector.tensor_copy(eds_g[:], eds_win[:].indirect(offsets[:]))
         nc.vector.quantize_mx(hd_c[:].bitcast(FP8X4), hd_s[:], hd_bf[:].rearrange("p q j -> p (q j)"))
 
         banks = [ps.tile([P, N], F32, name=f"bank{b}") for b in range(I // N)]
-        for b, z in [(2 * h + u, z) for h in range(2) for z in range(2) for u in range(2)]:
-            if True:
+        for z in range(2):
+            for b in range(I // N):
                 cols = slice(b * N, (b + 1) * N)
                 nc.tensor.matmul_mx(
                     banks[b][:],
@@ -122,7 +122,7 @@ def tile_attend_speculate_accept_kernel(tc, ht, hd, et_words, et_scales, ed_word
                     lhsT=hd_c[:].bitcast(FP8X4),
                     lhsT_scale=hd_s[:],
                     rhs=ed_g[h][:, u * N : (u + 1) * N].bitcast(FP8X4),
-                    rhs_scale=eds_g[:, b * N : (b + 1) * N],
+                    rhs_scale=eds_g[4:P, b * N : (b + 1) * N],
                     start=False,
                     stop=True,
                 )
@@ -132,5 +132,11 @@ def tile_attend_speculate_accept_kernel(tc, ht, hd, et_words, et_scales, ed_word
                     nc.vector.tensor_scalar(
                         excess[:, u * N : (u + 1) * N], banks[b][:], shift[:], 0.0, op0=ALU.add, op1=ALU.max
                     )
-            nc.scalar.activation(chance[:], excess[:], ACT.Exp, scale=-1.0)
-            nc.sync.dma_start(out[:, h * 2 * N : (h + 1) * 2 * N], chance[:])
+            if h == 0:
+                nc.scalar.activation(chance[:], excess[:], ACT.Exp, scale=-1.0)
+                nc.sync.dma_start(out[:, h * 2 * N : (h + 1) * 2 * N], chance[:])
+            else:
+                for u in range(2):
+                    b = 2 * h + u
+                    nc.scalar.activation(chance[:, u * N : (u + 1) * N], excess[:, u * N : (u + 1) * N], ACT.Exp, scale=-1.0)
+                    (nc.sync, nc.scalar)[u].dma_start(out[:, b * N : (b + 1) * N], chance[:, u * N : (u + 1) * N])

@@ -32,8 +32,8 @@ def tile_attend_speculate_accept_kernel(tc, ht, hd, et_words, et_scales, ed_word
         ed_win = sb.tile([P, T], U32, name="ed_win", align_bytes=64)
         ets_win = sb.tile([P, T], U8, name="ets_win", align_bytes=64)
         eds_win = sb.tile([P, T], U8, name="eds_win", align_bytes=64)
-        ht_raw = sb.tile([P, 2, PACK, Q], F32, name="ht_raw", align_bytes=64)
-        hd_raw = sb.tile([P, PACK, Q], F32, name="hd_raw", align_bytes=64)
+        ht_raw = sb.tile([P, 2, PACK, Q], F32, name="ht_raw", tag="ht_raw", align_bytes=64)
+        hd_raw = sb.tile([P, PACK, Q], F32, name="hd_raw", tag="hd_raw", align_bytes=64)
         l1_col = sb.tile([P, 1], F32, name="l1_col")
         l2_col = sb.tile([P, 1], F32, name="l2_col")
 
@@ -42,8 +42,6 @@ def tile_attend_speculate_accept_kernel(tc, ht, hd, et_words, et_scales, ed_word
         warm = sb.tile([P, 2], F32, name="warm")
         nc.gpsimd.memset(warm[:, 0:1], 0.0)
         nc.scalar.activation(warm[:, 1:2], warm[:, 0:1], ACT.Exp)
-        ets_g = [sb.tile([P, I], U8, name=f"ets_g{z}", align_bytes=64) for z in range(2)]
-        nc.gpsimd.memset(ets_g[1][:].bitcast(I32), 0)
 
         nc.gpsimd.dma_start(l1_col[:], l1)
         nc.gpsimd.dma_start(l2_col[:], l2)
@@ -62,8 +60,6 @@ def tile_attend_speculate_accept_kernel(tc, ht, hd, et_words, et_scales, ed_word
         nc.sync.dma_start(hd_raw[:], hd.rearrange("(p j) q -> p j q", j=PACK))
         nc.sync.dma_start(ed_win[:].bitcast(I32), ed_words[0].rearrange("p c r -> p (c r)").bitcast(I32))
 
-        shift = sb.tile([P, 1], F32, name="shift")
-        nc.gpsimd.tensor_tensor(shift[:], l1_col[:], l2_col[:], ALU.subtract)
 
         ht_bf = sb.tile([P, 2, Q, PACK], BF16, name="ht_bf", align_bytes=64)
         hd_bf = sb.tile([P, Q, PACK], BF16, name="hd_bf", align_bytes=64)
@@ -79,8 +75,14 @@ def tile_attend_speculate_accept_kernel(tc, ht, hd, et_words, et_scales, ed_word
             hd_raw[:].rearrange("p j (c i) -> p c j i", i=4),
             ACT.Copy,
         )
+        shift = sb.tile([P, 1], F32, name="shift", tag="hd_raw", align_bytes=64)
+        nc.scalar.activation(shift[:], l2_col[:], ACT.Identity, bias=l1_col[:], scale=-1.0)
 
         et_g = [sb.tile([P, I], U16, name=f"et_g{z}", align_bytes=64) for z in range(2)]
+        ets_g = [
+            sb.tile([P, I], U8, name="ets_g0", align_bytes=64),
+            sb.tile([P, I], U8, name="ets_g1", tag="ht_raw", align_bytes=64),
+        ]
         eds_g = sb.tile([P, I], U8, name="eds_g", align_bytes=64)
         ed_g = [sb.tile([P, I // 2], U32, name=f"ed_g{h}", align_bytes=64) for h in range(2)]
         ht_c = sb.tile([P, 2 * Q], U32, name="ht_c", align_bytes=64)
@@ -90,7 +92,7 @@ def tile_attend_speculate_accept_kernel(tc, ht, hd, et_words, et_scales, ed_word
 
         nc.vector.tensor_copy(et_g[0][:], et_win[0][:].indirect(offsets[:]))
         nc.vector.tensor_copy(ets_g[0][:], ets_win[:].indirect(offsets[:]))
-        nc.sync.dma_start(ets_g[1][0:100].bitcast(I32), ets_g[0][16:116].bitcast(I32))
+        nc.scalar.dma_start(ets_g[1][0:100].bitcast(I32), ets_g[0][16:116].bitcast(I32))
         nc.vector.tensor_copy(et_g[1][:], et_win[1][:].indirect(offsets[:]))
         nc.vector.quantize_mx(ht_c[:].bitcast(FP8X4), ht_s[:], ht_bf[:].rearrange("p z q j -> p (z q j)"))
         nc.vector.tensor_copy(eds_g[:], eds_win[:].indirect(offsets[:]))

@@ -43,9 +43,6 @@ def tile_attend_speculate_accept_kernel(tc, ht, hd, et_words, et_scales, ed_word
         nc.gpsimd.memset(warm[:, 0:1], 0.0)
         nc.scalar.activation(warm[:, 1:2], warm[:, 0:1], ACT.Exp)
 
-        nc.gpsimd.dma_start(l1_col[:], l1)
-        nc.gpsimd.dma_start(l2_col[:], l2)
-
         nc.sync.dma_start(et_win[0][:].bitcast(I32), et_words[0].bitcast(I32))
         nc.sync.dma_start(offsets[:], offs)
         for r in range(4):
@@ -59,6 +56,8 @@ def tile_attend_speculate_accept_kernel(tc, ht, hd, et_words, et_scales, ed_word
             nc.sync.dma_start(eds_win[4 + r : P : 32].bitcast(I32), ed_scales[0, r:16:4, :].bitcast(I32))
         nc.sync.dma_start(hd_raw[:], hd.rearrange("(p j) q -> p j q", j=PACK))
         nc.sync.dma_start(ed_win[:].bitcast(I32), ed_words[0].rearrange("p c r -> p (c r)").bitcast(I32))
+        nc.sync.dma_start(l1_col[:], l1)
+        nc.sync.dma_start(l2_col[:], l2)
 
 
         ht_bf = sb.tile([P, 2, Q, PACK], BF16, name="ht_bf", align_bytes=64)
@@ -115,8 +114,8 @@ def tile_attend_speculate_accept_kernel(tc, ht, hd, et_words, et_scales, ed_word
         for h in range(2):
             nc.vector.tensor_copy(ed_g[h][:], ed_win[:].indirect(offsets[:, h * 16 : (h + 1) * 16]))
         for h in range(2):
-            excess = sb.tile([P, 2 * N], F32, name=f"excess{h}")
-            chance = sb.tile([P, 2 * N], F32, name=f"chance{h}")
+            excess = sb.tile([P, 2 * N], F32, name=f"excess{h}", tag=f"excess{h}")
+            chance = sb.tile([P, 2 * N], F32, name=f"chance{h}", tag=("chance0", "excess0")[h])
             for u in range(2):
                 b = 2 * h + u
                 nc.tensor.matmul_mx(

@@ -38,13 +38,14 @@ def tile_attend_speculate_accept_kernel(tc, ht, hd, et_words, et_scales, ed_word
         l2_col = sb.tile([P, 1], F32, name="l2_col")
 
         nc.vector.memset(ets_win[:].bitcast(I32), 0)
-        nc.vector.memset(eds_win[:].bitcast(I32), 0)
+        nc.vector.memset(eds_win[0:112].bitcast(I32), 0)
         warm = sb.tile([P, 2], F32, name="warm")
         nc.gpsimd.memset(warm[:, 0:1], 0.0)
         nc.scalar.activation(warm[:, 1:2], warm[:, 0:1], ACT.Exp)
 
-        nc.sync.dma_start(et_win[0][:].bitcast(I32), et_words[0].bitcast(I32))
         nc.sync.dma_start(offsets[:], offs)
+        nc.sync.dma_start(eds_win[112:P].bitcast(I32), ed_scales[0].bitcast(I32))
+        nc.sync.dma_start(et_win[0][:].bitcast(I32), et_words[0].bitcast(I32))
         for r in range(4):
             nc.sync.dma_start(
                 ets_win[r:P:16].bitcast(I32),
@@ -52,12 +53,8 @@ def tile_attend_speculate_accept_kernel(tc, ht, hd, et_words, et_scales, ed_word
             )
         nc.sync.dma_start(ht_raw[:], ht.rearrange("(z p j) q -> p z j q", z=2, j=PACK))
         nc.sync.dma_start(et_win[1][:].bitcast(I32), et_words[1].bitcast(I32))
-        for r in range(4):
-            nc.sync.dma_start(eds_win[4 + r : P : 32].bitcast(I32), ed_scales[0, r:16:4, :].bitcast(I32))
         nc.sync.dma_start(hd_raw[:], hd.rearrange("(p j) q -> p j q", j=PACK))
         nc.sync.dma_start(ed_win[:].bitcast(I32), ed_words[0].rearrange("p c r -> p (c r)").bitcast(I32))
-        nc.sync.dma_start(l1_col[:], l1)
-        nc.sync.dma_start(l2_col[:], l2)
 
 
         ht_bf = sb.tile([P, 2, Q, PACK], BF16, name="ht_bf", align_bytes=64)
@@ -74,8 +71,6 @@ def tile_attend_speculate_accept_kernel(tc, ht, hd, et_words, et_scales, ed_word
             hd_raw[:].rearrange("p j (c i) -> p c j i", i=4),
             ACT.Copy,
         )
-        shift = sb.tile([P, 1], F32, name="shift", tag="hd_raw", align_bytes=64)
-        nc.scalar.activation(shift[:], l2_col[:], ACT.Identity, bias=l1_col[:], scale=-1.0)
 
         et_g = [sb.tile([P, I], U16, name=f"et_g{z}", align_bytes=64) for z in range(2)]
         ets_g = [
@@ -89,12 +84,22 @@ def tile_attend_speculate_accept_kernel(tc, ht, hd, et_words, et_scales, ed_word
         hd_c = sb.tile([P, Q], U32, name="hd_c", align_bytes=64)
         hd_s = sb.tile([P, Q], U8, name="hd_s", align_bytes=64)
 
+        eds_rows = sb.tile([P, I], U8, name="eds_rows", align_bytes=64)
+        nc.vector.tensor_copy(eds_rows[:], eds_win[:].indirect(offsets[:]))
+        for a in range(4):
+            nc.sync.dma_start(
+                eds_g[32 * a + 4 : 32 * a + 8].bitcast(I32), eds_rows[112 + 4 * a : 116 + 4 * a].bitcast(I32)
+            )
+        nc.sync.dma_start(l1_col[:], l1)
+        nc.sync.dma_start(l2_col[:], l2)
+        shift = sb.tile([P, 1], F32, name="shift", tag="hd_raw", align_bytes=64)
+        nc.scalar.activation(shift[:], l1_col[:], ACT.Identity, bias=l2_col[:], scale=-1.0)
+
         nc.vector.tensor_copy(et_g[0][:], et_win[0][:].indirect(offsets[:]))
         nc.vector.tensor_copy(ets_g[0][:], ets_win[:].indirect(offsets[:]))
         nc.scalar.dma_start(ets_g[1][0:100].bitcast(I32), ets_g[0][16:116].bitcast(I32))
         nc.vector.tensor_copy(et_g[1][:], et_win[1][:].indirect(offsets[:]))
         nc.vector.quantize_mx(ht_c[:].bitcast(FP8X4), ht_s[:], ht_bf[:].rearrange("p z q j -> p (z q j)"))
-        nc.vector.tensor_copy(eds_g[:], eds_win[:].indirect(offsets[:]))
         nc.vector.quantize_mx(hd_c[:].bitcast(FP8X4), hd_s[:], hd_bf[:].rearrange("p q j -> p (q j)"))
 
         banks = [ps.tile([P, N], F32, name=f"bank{b}") for b in range(I // N)]
@@ -113,31 +118,21 @@ def tile_attend_speculate_accept_kernel(tc, ht, hd, et_words, et_scales, ed_word
 
         for h in range(2):
             nc.vector.tensor_copy(ed_g[h][:], ed_win[:].indirect(offsets[:, h * 16 : (h + 1) * 16]))
-        for h in range(2):
-            excess = sb.tile([P, 2 * N], F32, name=f"excess{h}", tag=f"excess{h}")
-            chance = sb.tile([P, 2 * N], F32, name=f"chance{h}", tag=("chance0", "excess0")[h])
-            for u in range(2):
-                b = 2 * h + u
-                nc.tensor.matmul_mx(
-                    banks[b][:],
-                    lhsT=hd_c[:].bitcast(FP8X4),
-                    lhsT_scale=hd_s[:],
-                    rhs=ed_g[h][:, u * N : (u + 1) * N].bitcast(FP8X4),
-                    rhs_scale=eds_g[4:P, b * N : (b + 1) * N],
-                    start=False,
-                    stop=True,
-                )
-                if h == 0:
-                    nc.scalar.activation(excess[:, u * N : (u + 1) * N], banks[b][:], ACT.Relu, bias=shift[:])
-                else:
-                    nc.vector.tensor_scalar(
-                        excess[:, u * N : (u + 1) * N], banks[b][:], shift[:], 0.0, op0=ALU.add, op1=ALU.max
-                    )
-            if h == 0:
-                nc.scalar.activation(chance[:], excess[:], ACT.Exp, scale=-1.0)
-                nc.sync.dma_start(out[:, h * 2 * N : (h + 1) * 2 * N], chance[:])
-            else:
-                for u in range(2):
-                    b = 2 * h + u
-                    nc.scalar.activation(chance[:, u * N : (u + 1) * N], excess[:, u * N : (u + 1) * N], ACT.Exp, scale=-1.0)
-                    (nc.sync, nc.scalar)[u].dma_start(out[:, b * N : (b + 1) * N], chance[:, u * N : (u + 1) * N])
+        ratio = sb.tile([P, I], F32, name="ratio")
+        chance = sb.tile([P, I], F32, name="chance")
+        for b in range(I // N):
+            h, u = divmod(b, 2)
+            cols = slice(b * N, (b + 1) * N)
+            nc.tensor.matmul_mx(
+                banks[b][:],
+                lhsT=hd_c[:].bitcast(FP8X4),
+                lhsT_scale=hd_s[:],
+                rhs=ed_g[h][:, u * N : (u + 1) * N].bitcast(FP8X4),
+                rhs_scale=eds_g[4:P, cols],
+                start=False,
+                stop=True,
+            )
+            nc.scalar.activation(ratio[:, cols], banks[b][:], ACT.Exp, bias=shift[:], scale=-1.0)
+        for cols, queue in ((slice(0, 2 * N), nc.sync), (slice(2 * N, 3 * N), nc.sync), (slice(3 * N, 4 * N), nc.scalar)):
+            nc.vector.tensor_scalar_min(chance[:, cols], ratio[:, cols], 1.0)
+            queue.dma_start(out[:, cols], chance[:, cols])

@@ -34,13 +34,14 @@ def tile_attend_speculate_accept_kernel(tc, ht, hd, et_words, et_scales, ed_word
         eds_win = sb.tile([P, T], U8, name="eds_win", align_bytes=64)
         ht_raw = sb.tile([P, 2, PACK, Q], F32, name="ht_raw", tag="ht_raw", align_bytes=64)
         hd_raw = sb.tile([P, PACK, Q], F32, name="hd_raw", tag="hd_raw", align_bytes=64)
-        l1_col = sb.tile([P, 1], F32, name="l1_col")
-        l2_col = sb.tile([P, 1], F32, name="l2_col")
+        l_rows = sb.tile([P, 32], F32, name="l_rows", align_bytes=64)
+        l_cols = sb.tile([P, 32], F32, name="l_cols", align_bytes=64)
 
         nc.vector.memset(ets_win[:].bitcast(I32), 0)
         nc.vector.memset(eds_win[0:112].bitcast(I32), 0)
         warm = sb.tile([P, 2], F32, name="warm")
-        nc.gpsimd.memset(warm[:, 0:1], 0.0)
+        nc.vector.memset(l_rows[:], 0.0)
+        nc.vector.memset(warm[:, 0:1], 0.0)
         nc.scalar.activation(warm[:, 1:2], warm[:, 0:1], ACT.Exp)
 
         nc.sync.dma_start(offsets[:], offs)
@@ -54,6 +55,8 @@ def tile_attend_speculate_accept_kernel(tc, ht, hd, et_words, et_scales, ed_word
         nc.sync.dma_start(ht_raw[:], ht.rearrange("(z p j) q -> p z j q", z=2, j=PACK))
         nc.sync.dma_start(et_win[1][:].bitcast(I32), et_words[1].bitcast(I32))
         nc.sync.dma_start(hd_raw[:], hd.rearrange("(p j) q -> p j q", j=PACK))
+        nc.sync.dma_start(l_rows[0:P:32], l1.rearrange("(a c) o -> a (c o)", a=4))
+        nc.sync.dma_start(l_rows[1:P:32], l2.rearrange("(a c) o -> a (c o)", a=4))
         nc.sync.dma_start(ed_win[:].bitcast(I32), ed_words[0].rearrange("p c r -> p (c r)").bitcast(I32))
 
 
@@ -90,10 +93,6 @@ def tile_attend_speculate_accept_kernel(tc, ht, hd, et_words, et_scales, ed_word
             nc.sync.dma_start(
                 eds_g[32 * a + 4 : 32 * a + 8].bitcast(I32), eds_rows[112 + 4 * a : 116 + 4 * a].bitcast(I32)
             )
-        nc.sync.dma_start(l1_col[:], l1)
-        nc.sync.dma_start(l2_col[:], l2)
-        shift = sb.tile([P, 1], F32, name="shift", tag="hd_raw", align_bytes=64)
-        nc.scalar.activation(shift[:], l1_col[:], ACT.Identity, bias=l2_col[:], scale=-1.0)
 
         nc.vector.tensor_copy(et_g[0][:], et_win[0][:].indirect(offsets[:]))
         nc.vector.tensor_copy(ets_g[0][:], ets_win[:].indirect(offsets[:]))
@@ -101,6 +100,10 @@ def tile_attend_speculate_accept_kernel(tc, ht, hd, et_words, et_scales, ed_word
         nc.vector.tensor_copy(et_g[1][:], et_win[1][:].indirect(offsets[:]))
         nc.vector.quantize_mx(ht_c[:].bitcast(FP8X4), ht_s[:], ht_bf[:].rearrange("p z q j -> p (z q j)"))
         nc.vector.quantize_mx(hd_c[:].bitcast(FP8X4), hd_s[:], hd_bf[:].rearrange("p q j -> p (q j)"))
+
+        shift = sb.tile([P, 1], F32, name="shift")
+        nc.vector.transpose(l_cols[:], l_rows[:])
+        nc.scalar.activation(shift[:], l_cols[:, 0:1], ACT.Identity, bias=l_cols[:, 1:2], scale=-1.0)
 
         banks = [ps.tile([P, N], F32, name=f"bank{b}") for b in range(I // N)]
         for z in range(2):

@@ -60,11 +60,11 @@ def tile_attend_speculate_accept_kernel(tc, ht, hd, et_words, et_scales, ed_word
         nc.sync.dma_start(ed_win[:].bitcast(I32), ed_words[0].rearrange("p c r -> p (c r)").bitcast(I32))
 
 
-        ht_bf = sb.tile([P, 2, Q, PACK], BF16, name="ht_bf", align_bytes=64)
+        ht_bf = [sb.tile([P, Q, PACK], BF16, name=f"ht_bf{z}", tag=f"ht_bf{z}", align_bytes=64) for z in range(2)]
         hd_bf = sb.tile([P, Q, PACK], BF16, name="hd_bf", align_bytes=64)
         for z in range(2):
             nc.scalar.activation(
-                ht_bf[:, z].rearrange("p (c i) j -> p c j i", i=4),
+                ht_bf[z][:].rearrange("p (c i) j -> p c j i", i=4),
                 ht_raw[:, z].rearrange("p j (c i) -> p c j i", i=4),
                 ACT.Copy,
                 scale=-1.0,
@@ -75,15 +75,15 @@ def tile_attend_speculate_accept_kernel(tc, ht, hd, et_words, et_scales, ed_word
             ACT.Copy,
         )
 
-        et_g = [sb.tile([P, I], U16, name=f"et_g{z}", align_bytes=64) for z in range(2)]
+        et_g = [sb.tile([P, I], U16, name="et_g0", align_bytes=64)]
         ets_g = [
             sb.tile([P, I], U8, name="ets_g0", align_bytes=64),
             sb.tile([P, I], U8, name="ets_g1", tag="ht_raw", align_bytes=64),
         ]
         eds_g = sb.tile([P, I], U8, name="eds_g", align_bytes=64)
         ed_g = [sb.tile([P, I // 2], U32, name=f"ed_g{h}", align_bytes=64) for h in range(2)]
-        ht_c = sb.tile([P, 2 * Q], U32, name="ht_c", align_bytes=64)
-        ht_s = sb.tile([P, 2 * Q], U8, name="ht_s", align_bytes=64)
+        ht_c = [sb.tile([P, Q], U32, name=f"ht_c{z}", align_bytes=64) for z in range(2)]
+        ht_s = [sb.tile([P, Q], U8, name=f"ht_s{z}", align_bytes=64) for z in range(2)]
         hd_c = sb.tile([P, Q], U32, name="hd_c", align_bytes=64)
         hd_s = sb.tile([P, Q], U8, name="hd_s", align_bytes=64)
 
@@ -96,9 +96,14 @@ def tile_attend_speculate_accept_kernel(tc, ht, hd, et_words, et_scales, ed_word
 
         nc.vector.tensor_copy(et_g[0][:], et_win[0][:].indirect(offsets[:]))
         nc.vector.tensor_copy(ets_g[0][:], ets_win[:].indirect(offsets[:]))
-        nc.scalar.dma_start(ets_g[1][0:100].bitcast(I32), ets_g[0][16:116].bitcast(I32))
+        for first, count in ((32, 64), (0, 4), (96, 4)):
+            nc.scalar.dma_start(
+                ets_g[1][first : first + count].bitcast(I32), ets_g[0][16 + first : 16 + first + count].bitcast(I32)
+            )
+        nc.vector.quantize_mx(ht_c[0][:].bitcast(FP8X4), ht_s[0][:], ht_bf[0][:].rearrange("p q j -> p (q j)"))
+        et_g.append(sb.tile([P, I], U16, name="et_g1", tag="ht_bf0", align_bytes=64))
         nc.vector.tensor_copy(et_g[1][:], et_win[1][:].indirect(offsets[:]))
-        nc.vector.quantize_mx(ht_c[:].bitcast(FP8X4), ht_s[:], ht_bf[:].rearrange("p z q j -> p (z q j)"))
+        nc.vector.quantize_mx(ht_c[1][:].bitcast(FP8X4), ht_s[1][:], ht_bf[1][:].rearrange("p q j -> p (q j)"))
         nc.vector.quantize_mx(hd_c[:].bitcast(FP8X4), hd_s[:], hd_bf[:].rearrange("p q j -> p (q j)"))
 
         shift = sb.tile([P, 1], F32, name="shift")
@@ -111,8 +116,8 @@ def tile_attend_speculate_accept_kernel(tc, ht, hd, et_words, et_scales, ed_word
                 cols = slice(b * N, (b + 1) * N)
                 nc.tensor.matmul_mx(
                     banks[b][:],
-                    lhsT=ht_c[:, z * Q : (z + 1) * Q].bitcast(FP8X4),
-                    lhsT_scale=ht_s[:, z * Q : (z + 1) * Q],
+                    lhsT=ht_c[z][:].bitcast(FP8X4),
+                    lhsT_scale=ht_s[z][:],
                     rhs=et_g[z][:, cols].bitcast(FP4X4),
                     rhs_scale=ets_g[z][:, cols],
                     start=(z == 0),

@@ -14,11 +14,14 @@ U8 = mybir.dt.uint8
 FP8X4 = mybir.dt.float8_e4m3fn_x4
 FP4X4 = mybir.dt.float4_e2m1fn_x4
 ACT = mybir.ActivationFunctionType
-ALU = mybir.AluOpType
 
 P = 128
 PACK = 4
+QUAD = 32
 N = 128
+ET1_ROWS = 16
+ED_ROWS = 112
+ED_PLANE = 4
 
 
 def tile_attend_speculate_accept_kernel(tc, ht, hd, et_words, et_scales, ed_words, ed_scales, l1, l2, offs, out):
@@ -28,37 +31,35 @@ def tile_attend_speculate_accept_kernel(tc, ht, hd, et_words, et_scales, ed_word
         ps = ctx.enter_context(tc.psum_pool(name="ps", bufs=1))
 
         offsets = sb.tile([P, I // 16], U16, name="offsets")
-        et_win = [sb.tile([P, T], U16, name=f"et_win{z}", tag=f"et_win{z}", align_bytes=64) for z in range(2)]
+        et_win = [sb.tile([P, T], U16, name=f"et_win{z}", align_bytes=64) for z in range(2)]
         ed_win = sb.tile([P, T], U32, name="ed_win", align_bytes=64)
         ets_win = sb.tile([P, T], U8, name="ets_win", align_bytes=64)
         eds_win = sb.tile([P, T], U8, name="eds_win", align_bytes=64)
         ht_raw = sb.tile([P, 2, PACK, Q], F32, name="ht_raw", tag="ht_raw", align_bytes=64)
-        hd_raw = sb.tile([P, PACK, Q], F32, name="hd_raw", tag="hd_raw", align_bytes=64)
-        l_rows = sb.tile([P, 32], F32, name="l_rows", align_bytes=64)
-        l_cols = sb.tile([P, 32], F32, name="l_cols", align_bytes=64)
+        hd_raw = sb.tile([P, PACK, Q], F32, name="hd_raw", align_bytes=64)
+        l_rows = sb.tile([P, QUAD], F32, name="l_rows", align_bytes=64)
+        l_cols = sb.tile([P, QUAD], F32, name="l_cols", align_bytes=64)
 
         nc.vector.memset(ets_win[:].bitcast(I32), 0)
-        nc.vector.memset(eds_win[0:112].bitcast(I32), 0)
+        nc.vector.memset(eds_win[0:ED_ROWS].bitcast(I32), 0)
         warm = sb.tile([P, 2], F32, name="warm")
         nc.vector.memset(l_rows[:], 0.0)
         nc.vector.memset(warm[:, 0:1], 0.0)
         nc.scalar.activation(warm[:, 1:2], warm[:, 0:1], ACT.Exp)
 
         nc.sync.dma_start(offsets[:], offs)
-        nc.sync.dma_start(eds_win[112:P].bitcast(I32), ed_scales[0].bitcast(I32))
+        nc.scalar.dma_start(eds_win[ED_ROWS:P].bitcast(I32), ed_scales[0].bitcast(I32))
         nc.sync.dma_start(et_win[0][:].bitcast(I32), et_words[0].bitcast(I32))
         for r in range(4):
             nc.sync.dma_start(
-                ets_win[r:P:16].bitcast(I32),
+                ets_win[r:P:ET1_ROWS].bitcast(I32),
                 et_scales[:, r:16:4, :].rearrange("z a c -> a z c").bitcast(I32),
             )
         nc.sync.dma_start(ht_raw[:], ht.rearrange("(z p j) q -> p z j q", z=2, j=PACK))
         nc.sync.dma_start(et_win[1][:].bitcast(I32), et_words[1].bitcast(I32))
         nc.sync.dma_start(hd_raw[:], hd.rearrange("(p j) q -> p j q", j=PACK))
-        nc.sync.dma_start(l_rows[0:P:32], l1.rearrange("(a c) o -> a (c o)", a=4))
-        nc.sync.dma_start(l_rows[1:P:32], l2.rearrange("(a c) o -> a (c o)", a=4))
-        nc.sync.dma_start(ed_win[:].bitcast(I32), ed_words[0].rearrange("p c r -> p (c r)").bitcast(I32))
-
+        nc.sync.dma_start(l_rows[0:P:QUAD], l1.rearrange("(a c) o -> a (c o)", a=4))
+        nc.sync.dma_start(l_rows[1:P:QUAD], l2.rearrange("(a c) o -> a (c o)", a=4))
 
         ht_bf = [sb.tile([P, Q, PACK], BF16, name=f"ht_bf{z}", tag=f"ht_bf{z}", align_bytes=64) for z in range(2)]
         hd_bf = sb.tile([P, Q, PACK], BF16, name="hd_bf", align_bytes=64)
@@ -75,34 +76,34 @@ def tile_attend_speculate_accept_kernel(tc, ht, hd, et_words, et_scales, ed_word
             ACT.Copy,
         )
 
-        et_g = [sb.tile([P, I], U16, name="et_g0", align_bytes=64)]
-        ets_g = [
-            sb.tile([P, I], U8, name="ets_g0", align_bytes=64),
-            sb.tile([P, I], U8, name="ets_g1", tag="ht_raw", align_bytes=64),
-        ]
-        eds_g = sb.tile([P, I], U8, name="eds_g", align_bytes=64)
+        et0_g = sb.tile([P, I], U16, name="et0_g", align_bytes=64)
+        et0_plane = sb.tile([P, I], U8, name="et0_plane", align_bytes=64)
+        et1_plane = sb.tile([P, I], U8, name="et1_plane", tag="ht_raw", align_bytes=64)
+        ed_plane = sb.tile([P, I], U8, name="ed_plane", align_bytes=64)
         ed_g = [sb.tile([P, I // 2], U32, name=f"ed_g{h}", align_bytes=64) for h in range(2)]
         ht_c = [sb.tile([P, Q], U32, name=f"ht_c{z}", align_bytes=64) for z in range(2)]
         ht_s = [sb.tile([P, Q], U8, name=f"ht_s{z}", align_bytes=64) for z in range(2)]
         hd_c = sb.tile([P, Q], U32, name="hd_c", align_bytes=64)
         hd_s = sb.tile([P, Q], U8, name="hd_s", align_bytes=64)
+        eds_g = sb.tile([P, I], U8, name="eds_g", align_bytes=64)
 
-        eds_rows = sb.tile([P, I], U8, name="eds_rows", align_bytes=64)
-        nc.vector.tensor_copy(eds_rows[:], eds_win[:].indirect(offsets[:]))
-        for a in range(4):
-            nc.sync.dma_start(
-                eds_g[32 * a + 4 : 32 * a + 8].bitcast(I32), eds_rows[112 + 4 * a : 116 + 4 * a].bitcast(I32)
-            )
+        def move_ed_scale_rows(a):
+            to, come = QUAD * a + ED_PLANE, ED_ROWS + 4 * a
+            nc.sync.dma_start(ed_plane[to : to + 4].bitcast(I32), eds_g[come : come + 4].bitcast(I32))
 
-        nc.vector.tensor_copy(et_g[0][:], et_win[0][:].indirect(offsets[:]))
-        nc.vector.tensor_copy(ets_g[0][:], ets_win[:].indirect(offsets[:]))
-        for first, count in ((32, 64), (0, 4), (96, 4)):
-            nc.scalar.dma_start(
-                ets_g[1][first : first + count].bitcast(I32), ets_g[0][16 + first : 16 + first + count].bitcast(I32)
-            )
+        nc.vector.tensor_copy(eds_g[:], eds_win[:].indirect(offsets[:]))
+        move_ed_scale_rows(0)
+        nc.sync.dma_start(ed_win[:].bitcast(I32), ed_words[0].rearrange("p c r -> p (c r)").bitcast(I32))
+        for a in range(1, 4):
+            move_ed_scale_rows(a)
+
+        nc.vector.tensor_copy(et0_g[:], et_win[0][:].indirect(offsets[:]))
+        nc.vector.tensor_copy(et0_plane[:], ets_win[:].indirect(offsets[:]))
+        for r in range(4):
+            nc.scalar.dma_start(et1_plane[r:P:QUAD].bitcast(I32), et0_plane[ET1_ROWS + r : P : QUAD].bitcast(I32))
         nc.vector.quantize_mx(ht_c[0][:].bitcast(FP8X4), ht_s[0][:], ht_bf[0][:].rearrange("p q j -> p (q j)"))
-        et_g.append(sb.tile([P, I], U16, name="et_g1", tag="ht_bf0", align_bytes=64))
-        nc.vector.tensor_copy(et_g[1][:], et_win[1][:].indirect(offsets[:]))
+        et1_g = sb.tile([P, I], U16, name="et1_g", tag="ht_bf0", align_bytes=64)
+        nc.vector.tensor_copy(et1_g[:], et_win[1][:].indirect(offsets[:]))
         nc.vector.quantize_mx(ht_c[1][:].bitcast(FP8X4), ht_s[1][:], ht_bf[1][:].rearrange("p q j -> p (q j)"))
         nc.vector.quantize_mx(hd_c[:].bitcast(FP8X4), hd_s[:], hd_bf[:].rearrange("p q j -> p (q j)"))
 
@@ -111,15 +112,15 @@ def tile_attend_speculate_accept_kernel(tc, ht, hd, et_words, et_scales, ed_word
         nc.scalar.activation(shift[:], l_cols[:, 0:1], ACT.Identity, bias=l_cols[:, 1:2], scale=-1.0)
 
         banks = [ps.tile([P, N], F32, name=f"bank{b}") for b in range(I // N)]
-        for z in range(2):
+        for z, (et_g, et_plane) in enumerate(((et0_g, et0_plane), (et1_g, et1_plane))):
             for b in range(I // N):
                 cols = slice(b * N, (b + 1) * N)
                 nc.tensor.matmul_mx(
                     banks[b][:],
                     lhsT=ht_c[z][:].bitcast(FP8X4),
                     lhsT_scale=ht_s[z][:],
-                    rhs=et_g[z][:, cols].bitcast(FP4X4),
-                    rhs_scale=ets_g[z][:, cols],
+                    rhs=et_g[:, cols].bitcast(FP4X4),
+                    rhs_scale=et_plane[:, cols],
                     start=(z == 0),
                     stop=False,
                 )
@@ -136,7 +137,7 @@ def tile_attend_speculate_accept_kernel(tc, ht, hd, et_words, et_scales, ed_word
                 lhsT=hd_c[:].bitcast(FP8X4),
                 lhsT_scale=hd_s[:],
                 rhs=ed_g[h][:, u * N : (u + 1) * N].bitcast(FP8X4),
-                rhs_scale=eds_g[4:P, cols],
+                rhs_scale=ed_plane[ED_PLANE:P, cols],
                 start=False,
                 stop=True,
             )

@@ -19,8 +19,9 @@ P = 128
 PACK = 4
 QUAD = 32
 N = 128
-ET1_ROWS = 16
-ED_ROWS = 112
+ET_ROWS = 96
+ED_ROWS = 48
+ED_SPLIT = 512
 ED_PLANE = 4
 
 
@@ -36,30 +37,39 @@ def tile_attend_speculate_accept_kernel(tc, ht, hd, et_words, et_scales, ed_word
         ets_win = sb.tile([P, T], U8, name="ets_win", align_bytes=64)
         eds_win = sb.tile([P, T], U8, name="eds_win", align_bytes=64)
         ht_raw = sb.tile([P, 2, PACK, Q], F32, name="ht_raw", tag="ht_raw", align_bytes=64)
-        hd_raw = sb.tile([P, PACK, Q], F32, name="hd_raw", align_bytes=64)
+        hd_raw = sb.tile([P, PACK, Q], F32, name="hd_raw", tag="hd_raw", align_bytes=64)
         l_rows = sb.tile([P, QUAD], F32, name="l_rows", align_bytes=64)
         l_cols = sb.tile([P, QUAD], F32, name="l_cols", align_bytes=64)
 
-        nc.vector.memset(ets_win[:].bitcast(I32), 0)
-        nc.vector.memset(eds_win[0:ED_ROWS].bitcast(I32), 0)
         warm = sb.tile([P, 2], F32, name="warm")
         nc.vector.memset(l_rows[:], 0.0)
         nc.vector.memset(warm[:, 0:1], 0.0)
-        nc.scalar.activation(warm[:, 1:2], warm[:, 0:1], ACT.Exp)
+        nc.vector.memset(ets_win[0:ET_ROWS].bitcast(I32), 0)
+        nc.vector.memset(eds_win[0:ED_ROWS].bitcast(I32), 0)
+        nc.gpsimd.memset(eds_win[ED_ROWS + 16 : P].bitcast(I32), 0)
 
         nc.sync.dma_start(offsets[:], offs)
-        nc.scalar.dma_start(eds_win[ED_ROWS:P].bitcast(I32), ed_scales[0].bitcast(I32))
+        nc.scalar.dma_start(ets_win[ET_ROWS:P].bitcast(I32), et_scales.rearrange("z f c -> f z c").bitcast(I32))
+        nc.scalar.dma_start(eds_win[ED_ROWS : ED_ROWS + 16].bitcast(I32), ed_scales[0].bitcast(I32))
+        nc.scalar.activation(warm[:, 1:2], warm[:, 0:1], ACT.Exp)
         nc.sync.dma_start(et_win[0][:].bitcast(I32), et_words[0].bitcast(I32))
-        for r in range(4):
-            nc.sync.dma_start(
-                ets_win[r:P:ET1_ROWS].bitcast(I32),
-                et_scales[:, r:16:4, :].rearrange("z a c -> a z c").bitcast(I32),
-            )
+        nc.sync.dma_start(l_rows[0:P:QUAD], l1.rearrange("(a c) o -> a (c o)", a=4))
+        nc.sync.dma_start(l_rows[1:P:QUAD], l2.rearrange("(a c) o -> a (c o)", a=4))
         nc.sync.dma_start(ht_raw[:], ht.rearrange("(z p j) q -> p z j q", z=2, j=PACK))
         nc.sync.dma_start(et_win[1][:].bitcast(I32), et_words[1].bitcast(I32))
         nc.sync.dma_start(hd_raw[:], hd.rearrange("(p j) q -> p j q", j=PACK))
-        nc.sync.dma_start(l_rows[0:P:QUAD], l1.rearrange("(a c) o -> a (c o)", a=4))
-        nc.sync.dma_start(l_rows[1:P:QUAD], l2.rearrange("(a c) o -> a (c o)", a=4))
+        ed_dram = ed_words[0].rearrange("p c r -> p (c r)").bitcast(I32)
+        nc.sync.dma_start(ed_win[:, 0:ED_SPLIT].bitcast(I32), ed_dram[:, 0:ED_SPLIT])
+
+        ets_g = sb.tile([P, I], U8, name="ets_g", align_bytes=64)
+        et_planes = sb.tile([P, 2, I], U8, name="et_planes", align_bytes=64)
+        nc.vector.tensor_copy(ets_g[:], ets_win[:].indirect(offsets[:]))
+        for a in range(4):
+            nc.sync.dma_start(
+                et_planes[QUAD * a : QUAD * a + 4].rearrange("p z i -> p (z i)").bitcast(I32),
+                ets_g[ET_ROWS + 8 * a : ET_ROWS + 8 * a + 8].bitcast(I32),
+            )
+        nc.sync.dma_start(ed_win[:, ED_SPLIT:T].bitcast(I32), ed_dram[:, ED_SPLIT:T])
 
         ht_bf = [sb.tile([P, Q, PACK], BF16, name=f"ht_bf{z}", tag=f"ht_bf{z}", align_bytes=64) for z in range(2)]
         hd_bf = sb.tile([P, Q, PACK], BF16, name="hd_bf", align_bytes=64)
@@ -77,8 +87,6 @@ def tile_attend_speculate_accept_kernel(tc, ht, hd, et_words, et_scales, ed_word
         )
 
         et0_g = sb.tile([P, I], U16, name="et0_g", align_bytes=64)
-        et0_plane = sb.tile([P, I], U8, name="et0_plane", align_bytes=64)
-        et1_plane = sb.tile([P, I], U8, name="et1_plane", tag="ht_raw", align_bytes=64)
         ed_plane = sb.tile([P, I], U8, name="ed_plane", align_bytes=64)
         ed_g = [sb.tile([P, I // 2], U32, name=f"ed_g{h}", align_bytes=64) for h in range(2)]
         ht_c = [sb.tile([P, Q], U32, name=f"ht_c{z}", align_bytes=64) for z in range(2)]
@@ -92,27 +100,22 @@ def tile_attend_speculate_accept_kernel(tc, ht, hd, et_words, et_scales, ed_word
             nc.sync.dma_start(ed_plane[to : to + 4].bitcast(I32), eds_g[come : come + 4].bitcast(I32))
 
         nc.vector.tensor_copy(eds_g[:], eds_win[:].indirect(offsets[:]))
-        move_ed_scale_rows(0)
-        nc.sync.dma_start(ed_win[:].bitcast(I32), ed_words[0].rearrange("p c r -> p (c r)").bitcast(I32))
-        for a in range(1, 4):
+        for a in range(4):
             move_ed_scale_rows(a)
 
         nc.vector.tensor_copy(et0_g[:], et_win[0][:].indirect(offsets[:]))
-        nc.vector.tensor_copy(et0_plane[:], ets_win[:].indirect(offsets[:]))
-        for r in range(4):
-            nc.scalar.dma_start(et1_plane[r:P:QUAD].bitcast(I32), et0_plane[ET1_ROWS + r : P : QUAD].bitcast(I32))
         nc.vector.quantize_mx(ht_c[0][:].bitcast(FP8X4), ht_s[0][:], ht_bf[0][:].rearrange("p q j -> p (q j)"))
         et1_g = sb.tile([P, I], U16, name="et1_g", tag="ht_bf0", align_bytes=64)
         nc.vector.tensor_copy(et1_g[:], et_win[1][:].indirect(offsets[:]))
         nc.vector.quantize_mx(ht_c[1][:].bitcast(FP8X4), ht_s[1][:], ht_bf[1][:].rearrange("p q j -> p (q j)"))
         nc.vector.quantize_mx(hd_c[:].bitcast(FP8X4), hd_s[:], hd_bf[:].rearrange("p q j -> p (q j)"))
 
-        shift = sb.tile([P, 1], F32, name="shift")
+        shift = sb.tile([P, 1], F32, name="shift", tag="hd_raw", align_bytes=64)
         nc.vector.transpose(l_cols[:], l_rows[:])
         nc.scalar.activation(shift[:], l_cols[:, 0:1], ACT.Identity, bias=l_cols[:, 1:2], scale=-1.0)
 
         banks = [ps.tile([P, N], F32, name=f"bank{b}") for b in range(I // N)]
-        for z, (et_g, et_plane) in enumerate(((et0_g, et0_plane), (et1_g, et1_plane))):
+        for z, et_g in enumerate((et0_g, et1_g)):
             for b in range(I // N):
                 cols = slice(b * N, (b + 1) * N)
                 nc.tensor.matmul_mx(
@@ -120,7 +123,7 @@ def tile_attend_speculate_accept_kernel(tc, ht, hd, et_words, et_scales, ed_word
                     lhsT=ht_c[z][:].bitcast(FP8X4),
                     lhsT_scale=ht_s[z][:],
                     rhs=et_g[:, cols].bitcast(FP4X4),
-                    rhs_scale=et_plane[:, cols],
+                    rhs_scale=et_planes[:, z, cols],
                     start=(z == 0),
                     stop=False,
                 )

@@ -21,7 +21,6 @@ QUAD = 32
 N = 128
 ET_ROWS = 96
 ED_ROWS = 48
-ED_SPLIT = 512
 ED_PLANE = 4
 
 
@@ -38,11 +37,10 @@ def tile_attend_speculate_accept_kernel(tc, ht, hd, et_words, et_scales, ed_word
         eds_win = sb.tile([P, T], U8, name="eds_win", align_bytes=64)
         ht_raw = sb.tile([P, 2, PACK, Q], F32, name="ht_raw", tag="ht_raw", align_bytes=64)
         hd_raw = sb.tile([P, PACK, Q], F32, name="hd_raw", tag="hd_raw", align_bytes=64)
-        l_rows = sb.tile([P, QUAD], F32, name="l_rows", align_bytes=64)
-        l_cols = sb.tile([P, QUAD], F32, name="l_cols", align_bytes=64)
+        l1_col = sb.tile([P, 1], F32, name="l1_col")
+        l2_col = sb.tile([P, 1], F32, name="l2_col")
 
         warm = sb.tile([P, 2], F32, name="warm")
-        nc.vector.memset(l_rows[:], 0.0)
         nc.vector.memset(warm[:, 0:1], 0.0)
         nc.vector.memset(ets_win[0:ET_ROWS].bitcast(I32), 0)
         nc.vector.memset(eds_win[0:ED_ROWS].bitcast(I32), 0)
@@ -53,13 +51,10 @@ def tile_attend_speculate_accept_kernel(tc, ht, hd, et_words, et_scales, ed_word
         nc.scalar.dma_start(eds_win[ED_ROWS : ED_ROWS + 16].bitcast(I32), ed_scales[0].bitcast(I32))
         nc.scalar.activation(warm[:, 1:2], warm[:, 0:1], ACT.Exp)
         nc.sync.dma_start(et_win[0][:].bitcast(I32), et_words[0].bitcast(I32))
-        nc.sync.dma_start(l_rows[0:P:QUAD], l1.rearrange("(a c) o -> a (c o)", a=4))
-        nc.sync.dma_start(l_rows[1:P:QUAD], l2.rearrange("(a c) o -> a (c o)", a=4))
         nc.sync.dma_start(ht_raw[:], ht.rearrange("(z p j) q -> p z j q", z=2, j=PACK))
         nc.sync.dma_start(et_win[1][:].bitcast(I32), et_words[1].bitcast(I32))
         nc.sync.dma_start(hd_raw[:], hd.rearrange("(p j) q -> p j q", j=PACK))
         ed_dram = ed_words[0].rearrange("p c r -> p (c r)").bitcast(I32)
-        nc.sync.dma_start(ed_win[:, 0:ED_SPLIT].bitcast(I32), ed_dram[:, 0:ED_SPLIT])
 
         ets_g = sb.tile([P, I], U8, name="ets_g", align_bytes=64)
         et_planes = sb.tile([P, 2, I], U8, name="et_planes", align_bytes=64)
@@ -69,13 +64,13 @@ def tile_attend_speculate_accept_kernel(tc, ht, hd, et_words, et_scales, ed_word
                 et_planes[QUAD * a : QUAD * a + 4].rearrange("p z i -> p (z i)").bitcast(I32),
                 ets_g[ET_ROWS + 8 * a : ET_ROWS + 8 * a + 8].bitcast(I32),
             )
-        nc.sync.dma_start(ed_win[:, ED_SPLIT:T].bitcast(I32), ed_dram[:, ED_SPLIT:T])
+        nc.sync.dma_start(ed_win[:].bitcast(I32), ed_dram)
 
-        ht_bf = [sb.tile([P, Q, PACK], BF16, name=f"ht_bf{z}", tag=f"ht_bf{z}", align_bytes=64) for z in range(2)]
+        ht_bf = sb.tile([P, 2, Q, PACK], BF16, name="ht_bf", align_bytes=64)
         hd_bf = sb.tile([P, Q, PACK], BF16, name="hd_bf", align_bytes=64)
         for z in range(2):
             nc.scalar.activation(
-                ht_bf[z][:].rearrange("p (c i) j -> p c j i", i=4),
+                ht_bf[:, z].rearrange("p (c i) j -> p c j i", i=4),
                 ht_raw[:, z].rearrange("p j (c i) -> p c j i", i=4),
                 ACT.Copy,
                 scale=-1.0,
@@ -89,8 +84,8 @@ def tile_attend_speculate_accept_kernel(tc, ht, hd, et_words, et_scales, ed_word
         et0_g = sb.tile([P, I], U16, name="et0_g", align_bytes=64)
         ed_plane = sb.tile([P, I], U8, name="ed_plane", align_bytes=64)
         ed_g = [sb.tile([P, I // 2], U32, name=f"ed_g{h}", align_bytes=64) for h in range(2)]
-        ht_c = [sb.tile([P, Q], U32, name=f"ht_c{z}", align_bytes=64) for z in range(2)]
-        ht_s = [sb.tile([P, Q], U8, name=f"ht_s{z}", align_bytes=64) for z in range(2)]
+        ht_c = sb.tile([P, 2, Q], U32, name="ht_c", align_bytes=64)
+        ht_s = sb.tile([P, 2, Q], U8, name="ht_s", align_bytes=64)
         hd_c = sb.tile([P, Q], U32, name="hd_c", align_bytes=64)
         hd_s = sb.tile([P, Q], U8, name="hd_s", align_bytes=64)
         eds_g = sb.tile([P, I], U8, name="eds_g", align_bytes=64)
@@ -102,17 +97,21 @@ def tile_attend_speculate_accept_kernel(tc, ht, hd, et_words, et_scales, ed_word
         nc.vector.tensor_copy(eds_g[:], eds_win[:].indirect(offsets[:]))
         for a in range(4):
             move_ed_scale_rows(a)
+        nc.sync.dma_start(l1_col[:], l1)
+        nc.sync.dma_start(l2_col[:], l2)
 
         nc.vector.tensor_copy(et0_g[:], et_win[0][:].indirect(offsets[:]))
-        nc.vector.quantize_mx(ht_c[0][:].bitcast(FP8X4), ht_s[0][:], ht_bf[0][:].rearrange("p q j -> p (q j)"))
-        et1_g = sb.tile([P, I], U16, name="et1_g", tag="ht_bf0", align_bytes=64)
+        nc.vector.quantize_mx(
+            ht_c[:].rearrange("p z q -> p (z q)").bitcast(FP8X4),
+            ht_s[:].rearrange("p z q -> p (z q)"),
+            ht_bf[:].rearrange("p z q j -> p (z q j)"),
+        )
+        et1_g = sb.tile([P, I], U16, name="et1_g", align_bytes=64)
         nc.vector.tensor_copy(et1_g[:], et_win[1][:].indirect(offsets[:]))
-        nc.vector.quantize_mx(ht_c[1][:].bitcast(FP8X4), ht_s[1][:], ht_bf[1][:].rearrange("p q j -> p (q j)"))
         nc.vector.quantize_mx(hd_c[:].bitcast(FP8X4), hd_s[:], hd_bf[:].rearrange("p q j -> p (q j)"))
 
         shift = sb.tile([P, 1], F32, name="shift", tag="hd_raw", align_bytes=64)
-        nc.vector.transpose(l_cols[:], l_rows[:])
-        nc.scalar.activation(shift[:], l_cols[:, 0:1], ACT.Identity, bias=l_cols[:, 1:2], scale=-1.0)
+        nc.scalar.activation(shift[:], l1_col[:], ACT.Identity, bias=l2_col[:], scale=-1.0)
 
         banks = [ps.tile([P, N], F32, name=f"bank{b}") for b in range(I // N)]
         for z, et_g in enumerate((et0_g, et1_g)):
@@ -120,8 +119,8 @@ def tile_attend_speculate_accept_kernel(tc, ht, hd, et_words, et_scales, ed_word
                 cols = slice(b * N, (b + 1) * N)
                 nc.tensor.matmul_mx(
                     banks[b][:],
-                    lhsT=ht_c[z][:].bitcast(FP8X4),
-                    lhsT_scale=ht_s[z][:],
+                    lhsT=ht_c[:, z].bitcast(FP8X4),
+                    lhsT_scale=ht_s[:, z],
                     rhs=et_g[:, cols].bitcast(FP4X4),
                     rhs_scale=et_planes[:, z, cols],
                     start=(z == 0),

@@ -40,8 +40,6 @@ def tile_attend_speculate_accept_kernel(tc, ht, hd, et_words, et_scales, ed_word
         l1_col = sb.tile([P, 1], F32, name="l1_col")
         l2_col = sb.tile([P, 1], F32, name="l2_col")
 
-        warm = sb.tile([P, 2], F32, name="warm")
-        nc.vector.memset(warm[:, 0:1], 0.0)
         nc.vector.memset(ets_win[0:ET_ROWS].bitcast(I32), 0)
         nc.vector.memset(eds_win[0:ED_ROWS].bitcast(I32), 0)
         nc.gpsimd.memset(eds_win[ED_ROWS + 16 : P].bitcast(I32), 0)
@@ -49,7 +47,6 @@ def tile_attend_speculate_accept_kernel(tc, ht, hd, et_words, et_scales, ed_word
         nc.sync.dma_start(offsets[:], offs)
         nc.scalar.dma_start(ets_win[ET_ROWS:P].bitcast(I32), et_scales.rearrange("z f c -> f z c").bitcast(I32))
         nc.scalar.dma_start(eds_win[ED_ROWS : ED_ROWS + 16].bitcast(I32), ed_scales[0].bitcast(I32))
-        nc.scalar.activation(warm[:, 1:2], warm[:, 0:1], ACT.Exp)
         nc.sync.dma_start(et_win[0][:].bitcast(I32), et_words[0].bitcast(I32))
         nc.sync.dma_start(ht_raw[:], ht.rearrange("(z p j) q -> p z j q", z=2, j=PACK))
         nc.sync.dma_start(et_win[1][:].bitcast(I32), et_words[1].bitcast(I32))

@@ -19,9 +19,11 @@ P = 128
 PACK = 4
 QUAD = 32
 N = 128
+BLOCKS = 16
 ET_ROWS = 96
 ED_ROWS = 48
 ED_PLANE = 4
+HALF = I // 2
 
 
 def tile_attend_speculate_accept_kernel(tc, ht, hd, et_words, et_scales, ed_words, ed_scales, l1, l2, offs, out):
@@ -35,23 +37,22 @@ def tile_attend_speculate_accept_kernel(tc, ht, hd, et_words, et_scales, ed_word
         ed_win = sb.tile([P, T], U32, name="ed_win", align_bytes=64)
         ets_win = sb.tile([P, T], U8, name="ets_win", align_bytes=64)
         eds_win = sb.tile([P, T], U8, name="eds_win", align_bytes=64)
-        ht_raw = sb.tile([P, 2, PACK, Q], F32, name="ht_raw", tag="ht_raw", align_bytes=64)
+        ht_raw = sb.tile([P, 2, PACK, Q], F32, name="ht_raw", align_bytes=64)
         hd_raw = sb.tile([P, PACK, Q], F32, name="hd_raw", tag="hd_raw", align_bytes=64)
         l1_col = sb.tile([P, 1], F32, name="l1_col")
         l2_col = sb.tile([P, 1], F32, name="l2_col")
 
         nc.vector.memset(ets_win[0:ET_ROWS].bitcast(I32), 0)
         nc.vector.memset(eds_win[0:ED_ROWS].bitcast(I32), 0)
-        nc.gpsimd.memset(eds_win[ED_ROWS + 16 : P].bitcast(I32), 0)
+        nc.gpsimd.memset(eds_win[ED_ROWS + BLOCKS : P].bitcast(I32), 0)
 
         nc.sync.dma_start(offsets[:], offs)
         nc.scalar.dma_start(ets_win[ET_ROWS:P].bitcast(I32), et_scales.rearrange("z f c -> f z c").bitcast(I32))
-        nc.scalar.dma_start(eds_win[ED_ROWS : ED_ROWS + 16].bitcast(I32), ed_scales[0].bitcast(I32))
+        nc.scalar.dma_start(eds_win[ED_ROWS : ED_ROWS + BLOCKS].bitcast(I32), ed_scales[0].bitcast(I32))
         nc.sync.dma_start(et_win[0][:].bitcast(I32), et_words[0].bitcast(I32))
         nc.sync.dma_start(ht_raw[:], ht.rearrange("(z p j) q -> p z j q", z=2, j=PACK))
         nc.sync.dma_start(et_win[1][:].bitcast(I32), et_words[1].bitcast(I32))
         nc.sync.dma_start(hd_raw[:], hd.rearrange("(p j) q -> p j q", j=PACK))
-        ed_dram = ed_words[0].rearrange("p c r -> p (c r)").bitcast(I32)
 
         ets_g = sb.tile([P, I], U8, name="ets_g", align_bytes=64)
         et_planes = sb.tile([P, 2, I], U8, name="et_planes", align_bytes=64)
@@ -61,7 +62,9 @@ def tile_attend_speculate_accept_kernel(tc, ht, hd, et_words, et_scales, ed_word
                 et_planes[QUAD * a : QUAD * a + 4].rearrange("p z i -> p (z i)").bitcast(I32),
                 ets_g[ET_ROWS + 8 * a : ET_ROWS + 8 * a + 8].bitcast(I32),
             )
-        nc.sync.dma_start(ed_win[:].bitcast(I32), ed_dram)
+        nc.sync.dma_start(ed_win[:].bitcast(I32), ed_words[0].rearrange("p c r -> p (c r)").bitcast(I32))
+        nc.sync.dma_start(l1_col[:], l1)
+        nc.sync.dma_start(l2_col[:], l2)
 
         ht_bf = sb.tile([P, 2, Q, PACK], BF16, name="ht_bf", align_bytes=64)
         hd_bf = sb.tile([P, Q, PACK], BF16, name="hd_bf", align_bytes=64)
@@ -80,22 +83,17 @@ def tile_attend_speculate_accept_kernel(tc, ht, hd, et_words, et_scales, ed_word
 
         et0_g = sb.tile([P, I], U16, name="et0_g", align_bytes=64)
         ed_plane = sb.tile([P, I], U8, name="ed_plane", align_bytes=64)
-        ed_g = [sb.tile([P, I // 2], U32, name=f"ed_g{h}", align_bytes=64) for h in range(2)]
+        ed_g = [sb.tile([P, HALF], U32, name=f"ed_g{h}", align_bytes=64) for h in range(2)]
         ht_c = sb.tile([P, 2, Q], U32, name="ht_c", align_bytes=64)
         ht_s = sb.tile([P, 2, Q], U8, name="ht_s", align_bytes=64)
         hd_c = sb.tile([P, Q], U32, name="hd_c", align_bytes=64)
         hd_s = sb.tile([P, Q], U8, name="hd_s", align_bytes=64)
         eds_g = sb.tile([P, I], U8, name="eds_g", align_bytes=64)
 
-        def move_ed_scale_rows(a):
-            to, come = QUAD * a + ED_PLANE, ED_ROWS + 4 * a
-            nc.sync.dma_start(ed_plane[to : to + 4].bitcast(I32), eds_g[come : come + 4].bitcast(I32))
-
         nc.vector.tensor_copy(eds_g[:], eds_win[:].indirect(offsets[:]))
         for a in range(4):
-            move_ed_scale_rows(a)
-        nc.sync.dma_start(l1_col[:], l1)
-        nc.sync.dma_start(l2_col[:], l2)
+            to, come = QUAD * a + ED_PLANE, ED_ROWS + 4 * a
+            nc.sync.dma_start(ed_plane[to : to + 4].bitcast(I32), eds_g[come : come + 4].bitcast(I32))
 
         nc.vector.tensor_copy(et0_g[:], et_win[0][:].indirect(offsets[:]))
         nc.vector.quantize_mx(
@@ -125,7 +123,7 @@ def tile_attend_speculate_accept_kernel(tc, ht, hd, et_words, et_scales, ed_word
                 )
 
         for h in range(2):
-            nc.vector.tensor_copy(ed_g[h][:], ed_win[:].indirect(offsets[:, h * 16 : (h + 1) * 16]))
+            nc.vector.tensor_copy(ed_g[h][:], ed_win[:].indirect(offsets[:, h * HALF // 16 : (h + 1) * HALF // 16]))
         ratio = sb.tile([P, I], F32, name="ratio")
         chance = sb.tile([P, I], F32, name="chance")
         for b in range(I // N):

@@ -23,7 +23,7 @@ BLOCKS = 16
 ET_ROWS = 96
 ED_ROWS = 48
 ED_PLANE = 4
-HALF = I // 2
+ED_PIECES = (2 * N, N, N)
 
 
 def tile_attend_speculate_accept_kernel(tc, ht, hd, et_words, et_scales, ed_words, ed_scales, l1, l2, offs, out):
@@ -83,7 +83,7 @@ def tile_attend_speculate_accept_kernel(tc, ht, hd, et_words, et_scales, ed_word
 
         et0_g = sb.tile([P, I], U16, name="et0_g", align_bytes=64)
         ed_plane = sb.tile([P, I], U8, name="ed_plane", align_bytes=64)
-        ed_g = [sb.tile([P, HALF], U32, name=f"ed_g{h}", align_bytes=64) for h in range(2)]
+        ed_g = sb.tile([P, I], U32, name="ed_g", align_bytes=64)
         ht_c = sb.tile([P, 2, Q], U32, name="ht_c", align_bytes=64)
         ht_s = sb.tile([P, 2, Q], U8, name="ht_s", align_bytes=64)
         hd_c = sb.tile([P, Q], U32, name="hd_c", align_bytes=64)
@@ -122,18 +122,20 @@ def tile_attend_speculate_accept_kernel(tc, ht, hd, et_words, et_scales, ed_word
                     stop=False,
                 )
 
-        for h in range(2):
-            nc.vector.tensor_copy(ed_g[h][:], ed_win[:].indirect(offsets[:, h * HALF // 16 : (h + 1) * HALF // 16]))
+        first = 0
+        for count in ED_PIECES:
+            last = first + count
+            nc.vector.tensor_copy(ed_g[:, first:last], ed_win[:].indirect(offsets[:, first // 16 : last // 16]))
+            first = last
         ratio = sb.tile([P, I], F32, name="ratio")
         chance = sb.tile([P, I], F32, name="chance")
         for b in range(I // N):
-            h, u = divmod(b, 2)
             cols = slice(b * N, (b + 1) * N)
             nc.tensor.matmul_mx(
                 banks[b][:],
                 lhsT=hd_c[:].bitcast(FP8X4),
                 lhsT_scale=hd_s[:],
-                rhs=ed_g[h][:, u * N : (u + 1) * N].bitcast(FP8X4),
+                rhs=ed_g[:, cols].bitcast(FP8X4),
                 rhs_scale=ed_plane[ED_PLANE:P, cols],
                 start=False,
                 stop=True,

@@ -16,6 +16,7 @@ FP4X4 = mybir.dt.float4_e2m1fn_x4
 ACT = mybir.ActivationFunctionType
 
 P = 128
+ALIGN = 256
 PACK = 4
 QUAD = 32
 N = 128
@@ -32,13 +33,13 @@ def tile_attend_speculate_accept_kernel(tc, ht, hd, et_words, et_scales, ed_word
         sb = ctx.enter_context(tc.tile_pool(name="sb", bufs=1))
         ps = ctx.enter_context(tc.psum_pool(name="ps", bufs=1))
 
-        offsets = sb.tile([P, I // 16], U16, name="offsets")
-        et_win = [sb.tile([P, T], U16, name=f"et_win{z}", align_bytes=64) for z in range(2)]
-        ed_win = sb.tile([P, T], U32, name="ed_win", align_bytes=64)
-        ets_win = sb.tile([P, T], U8, name="ets_win", align_bytes=64)
-        eds_win = sb.tile([P, T], U8, name="eds_win", align_bytes=64)
-        ht_raw = sb.tile([P, 2, PACK, Q], F32, name="ht_raw", align_bytes=64)
-        hd_raw = sb.tile([P, PACK, Q], F32, name="hd_raw", tag="hd_raw", align_bytes=64)
+        offsets = sb.tile([P, I // 16], U16, name="offsets", align_bytes=ALIGN)
+        et_win = [sb.tile([P, T], U16, name=f"et_win{z}", align_bytes=ALIGN) for z in range(2)]
+        ed_win = sb.tile([P, T], U32, name="ed_win", align_bytes=ALIGN)
+        ets_win = sb.tile([P, T], U8, name="ets_win", align_bytes=ALIGN)
+        eds_win = sb.tile([P, T], U8, name="eds_win", align_bytes=ALIGN)
+        ht_raw = sb.tile([P, 2, PACK, Q], F32, name="ht_raw", align_bytes=ALIGN)
+        hd_raw = sb.tile([P, PACK, Q], F32, name="hd_raw", tag="hd_raw", align_bytes=ALIGN)
         l1_col = sb.tile([P, 1], F32, name="l1_col")
         l2_col = sb.tile([P, 1], F32, name="l2_col")
 
@@ -54,8 +55,8 @@ def tile_attend_speculate_accept_kernel(tc, ht, hd, et_words, et_scales, ed_word
         nc.sync.dma_start(et_win[1][:].bitcast(I32), et_words[1].bitcast(I32))
         nc.sync.dma_start(hd_raw[:], hd.rearrange("(p j) q -> p j q", j=PACK))
 
-        ets_g = sb.tile([P, I], U8, name="ets_g", align_bytes=64)
-        et_planes = sb.tile([P, 2, I], U8, name="et_planes", align_bytes=64)
+        ets_g = sb.tile([P, I], U8, name="ets_g", align_bytes=ALIGN)
+        et_planes = sb.tile([P, 2, I], U8, name="et_planes", align_bytes=ALIGN)
         nc.vector.tensor_copy(ets_g[:], ets_win[:].indirect(offsets[:]))
         for a in range(4):
             nc.sync.dma_start(
@@ -82,13 +83,13 @@ def tile_attend_speculate_accept_kernel(tc, ht, hd, et_words, et_scales, ed_word
         )
 
         et0_g = sb.tile([P, I], U16, name="et0_g", align_bytes=64)
-        ed_plane = sb.tile([P, I], U8, name="ed_plane", align_bytes=64)
+        ed_plane = sb.tile([P, I], U8, name="ed_plane", align_bytes=ALIGN)
         ed_g = sb.tile([P, I], U32, name="ed_g", align_bytes=64)
         ht_c = sb.tile([P, 2, Q], U32, name="ht_c", align_bytes=64)
         ht_s = sb.tile([P, 2, Q], U8, name="ht_s", align_bytes=64)
         hd_c = sb.tile([P, Q], U32, name="hd_c", align_bytes=64)
         hd_s = sb.tile([P, Q], U8, name="hd_s", align_bytes=64)
-        eds_g = sb.tile([P, I], U8, name="eds_g", align_bytes=64)
+        eds_g = sb.tile([P, I], U8, name="eds_g", align_bytes=ALIGN)
 
         nc.vector.tensor_copy(eds_g[:], eds_win[:].indirect(offsets[:]))
         for a in range(4):
@@ -105,7 +106,7 @@ def tile_attend_speculate_accept_kernel(tc, ht, hd, et_words, et_scales, ed_word
         nc.vector.tensor_copy(et1_g[:], et_win[1][:].indirect(offsets[:]))
         nc.vector.quantize_mx(hd_c[:].bitcast(FP8X4), hd_s[:], hd_bf[:].rearrange("p q j -> p (q j)"))
 
-        shift = sb.tile([P, 1], F32, name="shift", tag="hd_raw", align_bytes=64)
+        shift = sb.tile([P, 1], F32, name="shift", tag="hd_raw", align_bytes=ALIGN)
         nc.scalar.activation(shift[:], l1_col[:], ACT.Identity, bias=l2_col[:], scale=-1.0)
 
         banks = [ps.tile([P, N], F32, name=f"bank{b}") for b in range(I // N)]
@@ -128,7 +129,7 @@ def tile_attend_speculate_accept_kernel(tc, ht, hd, et_words, et_scales, ed_word
             nc.vector.tensor_copy(ed_g[:, first:last], ed_win[:].indirect(offsets[:, first // 16 : last // 16]))
             first = last
         ratio = sb.tile([P, I], F32, name="ratio")
-        chance = sb.tile([P, I], F32, name="chance")
+        chance = sb.tile([P, I], F32, name="chance", align_bytes=ALIGN)
         for b in range(I // N):
             cols = slice(b * N, (b + 1) * N)
             nc.tensor.matmul_mx(

@@ -64,8 +64,6 @@ def tile_attend_speculate_accept_kernel(tc, ht, hd, et_words, et_scales, ed_word
                 ets_g[ET_ROWS + 8 * a : ET_ROWS + 8 * a + 8].bitcast(I32),
             )
         nc.sync.dma_start(ed_win[:].bitcast(I32), ed_words[0].rearrange("p c r -> p (c r)").bitcast(I32))
-        nc.sync.dma_start(l1_col[:], l1)
-        nc.sync.dma_start(l2_col[:], l2)
 
         ht_bf = sb.tile([P, 2, Q, PACK], BF16, name="ht_bf", align_bytes=64)
         hd_bf = sb.tile([P, Q, PACK], BF16, name="hd_bf", align_bytes=64)
@@ -95,6 +93,8 @@ def tile_attend_speculate_accept_kernel(tc, ht, hd, et_words, et_scales, ed_word
         for a in range(4):
             to, come = QUAD * a + ED_PLANE, ED_ROWS + 4 * a
             nc.sync.dma_start(ed_plane[to : to + 4].bitcast(I32), eds_g[come : come + 4].bitcast(I32))
+        nc.sync.dma_start(l1_col[:], l1)
+        nc.sync.dma_start(l2_col[:], l2)
 
         nc.vector.tensor_copy(et0_g[:], et_win[0][:].indirect(offsets[:]))
         nc.vector.quantize_mx(

@@ -17,6 +17,7 @@ ACT = mybir.ActivationFunctionType
 
 P = 128
 ALIGN = 256
+PAGE = 4096
 PACK = 4
 QUAD = 32
 N = 128
@@ -34,11 +35,11 @@ def tile_attend_speculate_accept_kernel(tc, ht, hd, et_words, et_scales, ed_word
         ps = ctx.enter_context(tc.psum_pool(name="ps", bufs=1))
 
         offsets = sb.tile([P, I // 16], U16, name="offsets", align_bytes=ALIGN)
-        et_win = [sb.tile([P, T], U16, name=f"et_win{z}", align_bytes=ALIGN) for z in range(2)]
-        ed_win = sb.tile([P, T], U32, name="ed_win", align_bytes=ALIGN)
+        et_win = [sb.tile([P, T], U16, name=f"et_win{z}", align_bytes=PAGE) for z in range(2)]
+        ed_win = sb.tile([P, T], U32, name="ed_win", align_bytes=PAGE)
         ets_win = sb.tile([P, T], U8, name="ets_win", align_bytes=ALIGN)
         eds_win = sb.tile([P, T], U8, name="eds_win", align_bytes=ALIGN)
-        ht_raw = sb.tile([P, 2, PACK, Q], F32, name="ht_raw", align_bytes=ALIGN)
+        ht_raw = sb.tile([P, 2, PACK, Q], F32, name="ht_raw", align_bytes=PAGE)
         hd_raw = sb.tile([P, PACK, Q], F32, name="hd_raw", tag="hd_raw", align_bytes=ALIGN)
         l1_col = sb.tile([P, 1], F32, name="l1_col")
         l2_col = sb.tile([P, 1], F32, name="l2_col")

@@ -25,7 +25,7 @@ BLOCKS = 16
 ET_ROWS = 96
 ED_ROWS = 48
 ED_PLANE = 4
-ED_PIECES = (2 * N, N, N)
+ED_PIECES = (N, N, N, N)
 
 
 def tile_attend_speculate_accept_kernel(tc, ht, hd, et_words, et_scales, ed_words, ed_scales, l1, l2, offs, out):

@@ -39,10 +39,8 @@ def tile_attend_speculate_accept_kernel(tc, ht, hd, et_words, et_scales, ed_word
         ed_win = sb.tile([P, T], U32, name="ed_win", align_bytes=PAGE)
         ets_win = sb.tile([P, T], U8, name="ets_win", align_bytes=ALIGN)
         eds_win = sb.tile([P, T], U8, name="eds_win", align_bytes=ALIGN)
-        ht_raw = sb.tile([P, 2, PACK, Q], F32, name="ht_raw", align_bytes=PAGE)
+        ht_raw = sb.tile([P, 2, PACK, Q], F32, name="ht_raw", tag="ht_raw", align_bytes=PAGE)
         hd_raw = sb.tile([P, PACK, Q], F32, name="hd_raw", tag="hd_raw", align_bytes=ALIGN)
-        l1_col = sb.tile([P, 1], F32, name="l1_col")
-        l2_col = sb.tile([P, 1], F32, name="l2_col")
 
         nc.vector.memset(ets_win[0:ET_ROWS].bitcast(I32), 0)
         nc.vector.memset(eds_win[0:ED_ROWS].bitcast(I32), 0)
@@ -94,8 +92,6 @@ def tile_attend_speculate_accept_kernel(tc, ht, hd, et_words, et_scales, ed_word
         for a in range(4):
             to, come = QUAD * a + ED_PLANE, ED_ROWS + 4 * a
             nc.sync.dma_start(ed_plane[to : to + 4].bitcast(I32), eds_g[come : come + 4].bitcast(I32))
-        nc.sync.dma_start(l1_col[:], l1)
-        nc.sync.dma_start(l2_col[:], l2)
 
         nc.vector.tensor_copy(et0_g[:], et_win[0][:].indirect(offsets[:]))
         nc.vector.quantize_mx(
@@ -107,8 +103,12 @@ def tile_attend_speculate_accept_kernel(tc, ht, hd, et_words, et_scales, ed_word
         nc.vector.tensor_copy(et1_g[:], et_win[1][:].indirect(offsets[:]))
         nc.vector.quantize_mx(hd_c[:].bitcast(FP8X4), hd_s[:], hd_bf[:].rearrange("p q j -> p (q j)"))
 
+        lse = sb.tile([P, 2, 8], F32, name="lse", tag="ht_raw", align_bytes=PAGE)
+        nc.scalar.dma_start(lse[:, 0, 0:1], l1)
+        nc.scalar.dma_start(lse[:, 1, 0:1], l2)
+
         shift = sb.tile([P, 1], F32, name="shift", tag="hd_raw", align_bytes=ALIGN)
-        nc.scalar.activation(shift[:], l1_col[:], ACT.Identity, bias=l2_col[:], scale=-1.0)
+        nc.scalar.activation(shift[:], lse[:, 0, 0:1], ACT.Identity, bias=lse[:, 1, 0:1], scale=-1.0)
 
         banks = [ps.tile([P, N], F32, name=f"bank{b}") for b in range(I // N)]
         for z, et_g in enumerate((et0_g, et1_g)):

@@ -143,6 +143,6 @@ def tile_attend_speculate_accept_kernel(tc, ht, hd, et_words, et_scales, ed_word
                 stop=True,
             )
             nc.scalar.activation(ratio[:, cols], banks[b][:], ACT.Exp, bias=shift[:], scale=-1.0)
-        for cols, queue in ((slice(0, 2 * N), nc.sync), (slice(2 * N, 3 * N), nc.sync), (slice(3 * N, 4 * N), nc.scalar)):
+        for cols, queue in ((slice(0, 2 * N), nc.sync), (slice(2 * N, 3 * N), nc.scalar), (slice(3 * N, 4 * N), nc.sync)):
             nc.vector.tensor_scalar_min(chance[:, cols], ratio[:, cols], 1.0)
             queue.dma_start(out[:, cols], chance[:, cols])

from contextlib import ExitStack

import concourse.mybir as mybir

D, K, T, I, Q = 1024, 512, 2048, 512, 128
FLOPS = 2 * (D + K) * Q * I

F32 = mybir.dt.float32
BF16 = mybir.dt.bfloat16
I32 = mybir.dt.int32
U32 = mybir.dt.uint32
U16 = mybir.dt.uint16
U8 = mybir.dt.uint8
FP8X4 = mybir.dt.float8_e4m3fn_x4
FP4X4 = mybir.dt.float4_e2m1fn_x4
ACT = mybir.ActivationFunctionType

P = 128
ALIGN = 256
PAGE = 4096
PACK = 4
QUAD = 32
N = 128
BLOCKS = 16
ET_ROWS = 96
ED_ROWS = 48
ED_PLANE = 4
ED_PIECES = (N, N, N, N)


def tile_attend_speculate_accept_kernel(tc, ht, hd, et_words, et_scales, ed_words, ed_scales, l1, l2, offs, out):
    nc = tc.nc
    with ExitStack() as ctx:
        sb = ctx.enter_context(tc.tile_pool(name="sb", bufs=1))
        ps = ctx.enter_context(tc.psum_pool(name="ps", bufs=1))

        offsets = sb.tile([P, I // 16], U16, name="offsets", align_bytes=ALIGN)
        et_win = [sb.tile([P, T], U16, name=f"et_win{z}", align_bytes=PAGE) for z in range(2)]
        ed_win = sb.tile([P, T], U32, name="ed_win", align_bytes=PAGE)
        ets_win = sb.tile([P, T], U8, name="ets_win", align_bytes=ALIGN)
        eds_win = sb.tile([P, T], U8, name="eds_win", align_bytes=ALIGN)
        ht_raw = sb.tile([P, 2, PACK, Q], F32, name="ht_raw", tag="ht_raw", align_bytes=PAGE)
        hd_raw = sb.tile([P, PACK, Q], F32, name="hd_raw", tag="hd_raw", align_bytes=ALIGN)

        nc.vector.memset(ets_win[0:ET_ROWS].bitcast(I32), 0)
        nc.vector.memset(eds_win[0:ED_ROWS].bitcast(I32), 0)
        nc.gpsimd.memset(eds_win[ED_ROWS + BLOCKS : P].bitcast(I32), 0)

        nc.sync.dma_start(offsets[:], offs)
        nc.scalar.dma_start(ets_win[ET_ROWS:P].bitcast(I32), et_scales.rearrange("z f c -> f z c").bitcast(I32))
        nc.scalar.dma_start(eds_win[ED_ROWS : ED_ROWS + BLOCKS].bitcast(I32), ed_scales[0].bitcast(I32))
        nc.sync.dma_start(et_win[0][:].bitcast(I32), et_words[0].bitcast(I32))
        nc.sync.dma_start(ht_raw[:], ht.rearrange("(z p j) q -> p z j q", z=2, j=PACK))
        nc.sync.dma_start(et_win[1][:].bitcast(I32), et_words[1].bitcast(I32))
        nc.sync.dma_start(hd_raw[:], hd.rearrange("(p j) q -> p j q", j=PACK))

        ets_g = sb.tile([P, I], U8, name="ets_g", align_bytes=ALIGN)
        et_planes = sb.tile([P, 2, I], U8, name="et_planes", align_bytes=ALIGN)
        nc.vector.tensor_copy(ets_g[:], ets_win[:].indirect(offsets[:]))
        for a in range(4):
            nc.sync.dma_start(
                et_planes[QUAD * a : QUAD * a + 4].rearrange("p z i -> p (z i)").bitcast(I32),
                ets_g[ET_ROWS + 8 * a : ET_ROWS + 8 * a + 8].bitcast(I32),
            )
        nc.sync.dma_start(ed_win[:].bitcast(I32), ed_words[0].rearrange("p c r -> p (c r)").bitcast(I32))

        ht_bf = sb.tile([P, 2, Q, PACK], BF16, name="ht_bf", align_bytes=64)
        hd_bf = sb.tile([P, Q, PACK], BF16, name="hd_bf", align_bytes=64)
        for z in range(2):
            nc.scalar.activation(
                ht_bf[:, z].rearrange("p (c i) j -> p c j i", i=4),
                ht_raw[:, z].rearrange("p j (c i) -> p c j i", i=4),
                ACT.Copy,
                scale=-1.0,
            )
        nc.scalar.activation(
            hd_bf[:].rearrange("p (c i) j -> p c j i", i=4),
            hd_raw[:].rearrange("p j (c i) -> p c j i", i=4),
            ACT.Copy,
        )

        et0_g = sb.tile([P, I], U16, name="et0_g", align_bytes=64)
        ed_plane = sb.tile([P, I], U8, name="ed_plane", align_bytes=ALIGN)
        ed_g = sb.tile([P, I], U32, name="ed_g", align_bytes=64)
        ht_c = sb.tile([P, 2, Q], U32, name="ht_c", align_bytes=64)
        ht_s = sb.tile([P, 2, Q], U8, name="ht_s", align_bytes=64)
        hd_c = sb.tile([P, Q], U32, name="hd_c", align_bytes=64)
        hd_s = sb.tile([P, Q], U8, name="hd_s", align_bytes=64)
        eds_g = sb.tile([P, I], U8, name="eds_g", align_bytes=ALIGN)

        nc.vector.tensor_copy(eds_g[:], eds_win[:].indirect(offsets[:]))
        for a in range(4):
            to, come = QUAD * a + ED_PLANE, ED_ROWS + 4 * a
            nc.sync.dma_start(ed_plane[to : to + 4].bitcast(I32), eds_g[come : come + 4].bitcast(I32))

        nc.vector.tensor_copy(et0_g[:], et_win[0][:].indirect(offsets[:]))
        nc.vector.quantize_mx(
            ht_c[:].rearrange("p z q -> p (z q)").bitcast(FP8X4),
            ht_s[:].rearrange("p z q -> p (z q)"),
            ht_bf[:].rearrange("p z q j -> p (z q j)"),
        )
        et1_g = sb.tile([P, I], U16, name="et1_g", align_bytes=64)
        nc.vector.tensor_copy(et1_g[:], et_win[1][:].indirect(offsets[:]))
        nc.vector.quantize_mx(hd_c[:].bitcast(FP8X4), hd_s[:], hd_bf[:].rearrange("p q j -> p (q j)"))

        lse = sb.tile([P, 2, 8], F32, name="lse", tag="ht_raw", align_bytes=PAGE)
        nc.scalar.dma_start(lse[:, 0, 0:1], l1)
        nc.scalar.dma_start(lse[:, 1, 0:1], l2)

        shift = sb.tile([P, 1], F32, name="shift", tag="hd_raw", align_bytes=ALIGN)
        nc.scalar.activation(shift[:], lse[:, 0, 0:1], ACT.Identity, bias=lse[:, 1, 0:1], scale=-1.0)

        banks = [ps.tile([P, N], F32, name=f"bank{b}") for b in range(I // N)]
        for z, et_g in enumerate((et0_g, et1_g)):
            for b in range(I // N):
                cols = slice(b * N, (b + 1) * N)
                nc.tensor.matmul_mx(
                    banks[b][:],
                    lhsT=ht_c[:, z].bitcast(FP8X4),
                    lhsT_scale=ht_s[:, z],
                    rhs=et_g[:, cols].bitcast(FP4X4),
                    rhs_scale=et_planes[:, z, cols],
                    start=(z == 0),
                    stop=False,
                )

        first = 0
        for count in ED_PIECES:
            last = first + count
            nc.vector.tensor_copy(ed_g[:, first:last], ed_win[:].indirect(offsets[:, first // 16 : last // 16]))
            first = last
        ratio = sb.tile([P, I], F32, name="ratio")
        chance = sb.tile([P, I], F32, name="chance", align_bytes=ALIGN)
        for b in range(I // N):
            cols = slice(b * N, (b + 1) * N)
            nc.tensor.matmul_mx(
                banks[b][:],
                lhsT=hd_c[:].bitcast(FP8X4),
                lhsT_scale=hd_s[:],
                rhs=ed_g[:, cols].bitcast(FP8X4),
                rhs_scale=ed_plane[ED_PLANE:P, cols],
                start=False,
                stop=True,
            )
            nc.scalar.activation(ratio[:, cols], banks[b][:], ACT.Exp, bias=shift[:], scale=-1.0)
        for cols, queue in ((slice(0, 2 * N), nc.sync), (slice(2 * N, 3 * N), nc.scalar), (slice(3 * N, 4 * N), nc.sync)):
            nc.vector.tensor_scalar_min(chance[:, cols], ratio[:, cols], 1.0)
            queue.dma_start(out[:, cols], chance[:, cols])
